import numpy as np, ml_dtypes
CORES = [36,164,52,180,100,228,116,244]
N = 8
import mx_ref
BF = ml_dtypes.bfloat16
def gentries(a):
    return np.ascontiguousarray(a.reshape(8, 16, -1).transpose(0, 2, 1)).reshape(8, -1)
def gtable(e):
    e = np.asarray(e); return np.ascontiguousarray(e.reshape(8, -1, 16).transpose(0, 2, 1)).reshape(128, -1).astype(np.int32)
def gcols(t, e):
    v = np.concatenate([t.reshape(8, 16, -1, 4), np.zeros((8, 16, 1, 4), BF)], axis=2)
    return np.ascontiguousarray(np.stack([v[g][:, e[g]] for g in range(8)])).reshape(128, -1)
def tile(rs):
    return np.stack(rs, axis=2).reshape(128, -1).astype(BF)
def cut(t, i, w=512):
    return t[:, w * i:w * i + w]
def pick(q, e):
    c = np.concatenate([q[0].reshape(128, -1, 4), np.zeros((128, 1, 4), np.uint8)], axis=1); s = np.concatenate([q[1], np.ones((16, 1), np.uint8)], axis=1)
    return (np.ascontiguousarray(c[:, e].reshape(128, -1)), np.ascontiguousarray(s[:, e]))
def join(*qs):
    return (np.concatenate([q[0] for q in qs], axis=1), np.concatenate([q[1] for q in qs], axis=1))
def put(q, e, v):
    c, s = q[0].reshape(128, -1, 4).copy(), q[1].copy(); c[:, e] = v[0].reshape(128, -1, 4); s[:, e] = v[1]
    return (c.reshape(128, -1), s)
def pk(c, s):
    return (np.ascontiguousarray(c), mx_ref.live(s))
def emit(q):
    return q[0], q[1]
def packed(v, rng):
    q = [mx_ref.quantize(np.ascontiguousarray(v[r])) for r in range(N)]
    return np.stack([a for a, b in q]), np.stack([mx_ref.plane(b, rng) for a, b in q])
def values_of_codes():
    e, c = np.zeros((128, 128, 4), np.float32), np.zeros((128, 2, 4), np.uint8)
    e[np.arange(128), np.arange(128), 0] = 1
    c[:127, :, 0] = np.arange(256).reshape(2, 128).T[:127]
    return mx_ref.matmul(mx_ref.quantize(e.reshape(128, 512).astype(BF)), (c.reshape(128, 8), np.full((16, 2), 127, np.uint8))).T.reshape(-1).astype(np.float64)
CODE_VALUE, SCALE_VALUE = values_of_codes(), 2.0 ** (np.arange(256) - 127.0)
def decode(q):
    return (CODE_VALUE[q[0]].reshape(16, 8, -1, 4) * SCALE_VALUE[q[1]][:, None, :, None] + 0.0).reshape(128, -1).astype(np.float32)
def f(rng, *shape):
    return mx_ref.flush((rng.standard_normal(shape, dtype=np.float32) * np.exp2(rng.integers(-2, 3, shape[:-1] + (1,)))).astype(BF))
def wide(rng, *shape, cols=0):
    v = rng.standard_normal(shape, dtype=np.float32) * np.exp2(rng.integers(-12, 13, shape)).astype(np.float32)
    if cols: v *= np.repeat(np.exp2(rng.integers(-cols, cols + 1, shape[:-2] + (1, shape[-1] // 4))) * (rng.random(shape[:-2] + (1, shape[-1] // 4)) > 0.0625), 4, axis=-1).astype(np.float32)
    return mx_ref.flush(v.astype(BF))
C, A, R = 320, 64, 3
def order(p):
    return np.argsort(-(p + np.float32(0.0)), axis=1, kind="stable")
def means(t, a, x, b):
    return ((gcols(t, a).astype(np.float32) + gcols(x, b).astype(np.float32)) * np.float32(0.5)).astype(BF)
def along(o, e):
    return np.take_along_axis(o, e, axis=1)
def big(v):
    v = v.astype(np.float32)
    v[np.abs(v) < np.float32(2.0 ** -16)] = 0
    return v.astype(BF)
def families(rng):
    return np.stack([big(f(rng, N, 128, 4 * A)) for i in range(2)])
def lists_of(rng):
    return rng.integers(0, A, (2, N, 8, C)), rng.integers(0, C, (2, N, 8, C))
def others(rng):
    k = rng.integers(0, A - 8, (2, N, 8, C))
    return k + k // 7 + 1
def layers(rng, still=()):
    w = big(f(rng, N, 128, 2048)).reshape(N, 8, 16, 4, 8, 16, 4)
    for i in still:
        w[:, :, i] = 0
        w[:, :, :, :, :, i] = 0
    return w
def made(rng, x, s, a, b, w):
    c, p = packed(np.ascontiguousarray(w).reshape(N, 128, 2048), rng)
    x, s = np.ascontiguousarray(x).reshape(N, 128, 4 * C), np.ascontiguousarray(s).reshape(2, N, 128, 4 * A)
    t = [np.stack([gtable(e) for e in k]) for k in (a[0], b[0], a[1], b[1])]
    return {"x": x, "l0": s[0], "r0": s[1], "la": t[0], "lx": t[1], "ra": t[2], "rx": t[3], "wc": c, "ws": p, "v": np.array(f(rng, N, 128, 512))}
def signs(rng):
    return np.stack([rng.permutation(8) % 2 * 2.0 - 1.0 for r in range(N)])
def setup_inputs(rng):
    a, b = lists_of(rng)
    return made(rng, big(f(rng, N, 128, 4 * C)), families(rng), a, b, layers(rng))
def setup_inputs_ties(rng):
    x = big(f(rng, N, 128, 4 * C)).reshape(N, 8, 16, C, 4)
    s = families(rng).reshape(2, N, 8, 16, A, 4)
    keep = s[:, :, :, :8, 0].copy()
    e = rng.permutation(N)
    for r in range(N):
        for t in (x[r], s[0, r], s[1, r]):
            n = t.shape[2]
            k = np.zeros(n, int) if r == e[0] else rng.permutation(n) % 3
            m = t[:, :8, :3].copy()
            m[:, :, 2] = 0
            t[:, :8] = m[:, :, k]
    x[e[1]] = 0
    s[:, :, :, :, ::8] = 0
    for h in range(8): s[:, :, h, :8, 8 * h] = keep[:, :, h]
    a, b = lists_of(rng)
    return made(rng, x, s, a, b, layers(rng, range(8)))
def setup_inputs_near(rng):
    x, s = np.zeros((N, 8, 16, C, 4)), np.zeros((2, N, 8, 16, A, 4))
    a, b = others(rng), np.zeros((2, N, 8, C), int)
    o, c = rng.permutation(N) % 4, signs(rng)
    j = np.arange(C)
    g = ((((j + 1) // 2)[:, None] >> np.arange(8)) & 1) * np.exp2(np.arange(8) - 22.0)
    for r in range(N):
        size = 1.0 if o[r] < 2 else 2.0 ** -4
        if o[r] < 2:
            x[r, :, 0, :, 0] = 2 * c[r][:, None]
            for h in rng.permutation(8)[:4]: x[r, h, 0, C - 1 if c[r, h] > 0 else 0, 0] *= 2.0 ** 29
        if o[r] == 3: x[r, :, 0, :, 0] = (8 + j % 2) * 2.0 ** -29
        x[r, :, 8] = g[:, :4] * size
        x[r, :, 9] = g[:, 4:] * size
        x[r, :, 10:] = rng.integers(4, 8, (8, 6, C, 4)) * 2.0 ** -19 * size
        s[:, r, :, 10:] = rng.integers(4, 8, (2, 8, 6, A, 4)) * 2.0 ** -19 * size
        s[:, r, :, :, ::8] = 0
        k = 1.0 if o[r] == 0 else 2.0 ** -30
        for h in range(8):
            s[:, r, h, 0, 8 * h, 0] = k
            s[:, r, h, 8:10, 8 * h] = k
        m = rng.integers(0, C, (2, 8, 1))
        b[:, r] = (j + m) % (C // 2) * 2 + j // (C // 2) if o[r] == 3 else (j + m) % C
    return made(rng, x.astype(np.float32).astype(BF), s.astype(np.float32).astype(BF), a, b, layers(rng, range(10)))
def setup_inputs_huge(rng):
    one = rng.permutation(N) < N // 2
    n = N - N // 2
    def full(*shape):
        k = 1 - 0.04 * rng.random(shape + (4,))
        k[..., ::8, :, 0] = 1
        return k
    j = np.arange(C)
    c = np.where(one[:, None] | (j >= C // 2), -1.0, 1.0)
    x = 0.6 + 0.2 * rng.random((N, 128, C, 4))
    x[~one] = full(n, 128, C)
    x *= 2.0 ** 30 * c[:, None, :, None]
    s = -(0.6 + 0.2 * rng.random((2, N, 128, A, 4)))
    s[:, ~one] = full(2, n, 128, A) * np.where(np.arange(A) < A // 2, 1.0, -1.0)[:, None]
    q = 1 - 0.25 * rng.random((2, N, 128, 8, 4))
    q[:, ~one] = full(2, n, 128, 8)
    s[:, :, :, ::8] = q * np.stack([signs(rng), signs(rng)])[:, :, None, :, None]
    s *= 2.0 ** 30
    k = (np.argsort(rng.random((2, N, 1, C)), axis=3) >= A // 2).astype(int)
    b = k * (C // 2) + rng.integers(0, C // 2, (2, N, 8, C))
    m = rng.integers(0, A // 2 - 4, (2, N, 8, C))
    a = np.where(one[:, None, None], others(rng), k * (A // 2) + m + m // 7 + 1)
    w = np.zeros((N, 128, 4, 128, 4), np.float32)
    i = np.arange(128)
    for h in range(4): w[:, i, h, i, h] = -16
    return made(rng, x.astype(np.float32).astype(BF), s.astype(np.float32).astype(BF), a, b, w.astype(BF))
def setup_inputs_lists(rng):
    def shapes(n):
        i = np.arange(C)
        k = [np.zeros(C, int), np.full(C, n - 1), i % n, n - 1 - i % n, i * n // C, rng.permutation(C) % n, rng.permutation(n)[i % 2], rng.integers(0, n, C)]
        return np.stack(k)[rng.permutation(8)]
    a, b = [np.stack([np.stack([shapes(n) for r in range(N)]) for i in range(2)]) for n in (A, C)]
    e = int(rng.integers(N))
    a[:, e] = rng.integers(0, A, (2, 8, 1))
    b[:, e] = rng.integers(0, C, (2, 8, 1))
    return made(rng, big(f(rng, N, 128, 4 * C)), families(rng), a, b, layers(rng))
def setup_inputs_spread(rng):
    a, b = lists_of(rng)
    return made(rng, big(wide(rng, N, 128, 4 * C, cols=6)), np.stack([big(wide(rng, N, 128, 4 * A)) for i in range(2)]), a, b, layers(rng))
def check_inputs(d):
    b = []
    for k in ("x", "l0", "r0", "v"):
        a = np.abs(d[k].astype(np.float32))
        if not (np.isfinite(a).all() and ((a == 0) | (a >= 2.0 ** -30) & (a <= 2.0 ** 30)).all()): b.append("a value of " + k)
    for k, n in (("la", A), ("lx", C), ("ra", A), ("rx", C)):
        if not ((d[k] >= 0) & (d[k] < n)).all(): b.append("an entry of " + k)
    if ((d["wc"] & 0x7F) == 0x7F).any(): b.append("a code of wc that is no number")
    z = np.zeros((128, 4, 4), np.float32)
    z[:, 1] = 2.0 ** -30
    z[:, 2] = 2.0 ** 30
    c, s = emit(mx_ref.quantize(z.reshape(128, 16).astype(BF)))
    for r in range(N):
        p = mx_ref.live(d["ws"][r])
        if not ((p == s[0, 0]) | (p >= s[0, 1]) & (p <= s[0, 2])).all(): b.append("a scale of ws")
    return b
def reference(x, l0, r0, la, lx, ra, rx, wc, ws, v):
    lay = [pk(wc[r], ws[r]) for r in range(N)]
    left, right = [l0[r] for r in range(N)], [r0[r] for r in range(N)]
    ol = [np.tile(A * r + np.arange(A), (8, 1)) for r in range(N)]
    og = [k.copy() for k in ol]
    for t in range(R):
        sent, pl, pg = [], [], []
        for r in range(N):
            a, c = gentries(la[r]), gentries(ra[r])
            z, w = means(left[r], a, x[r], gentries(lx[r])), means(right[r], c, x[r], gentries(rx[r]))
            q = mx_ref.quantize(np.concatenate([right[r], left[r]], axis=1))
            e = order(mx_ref.matmul(q, mx_ref.quantize(z))[:A:8])[:, :A]
            h = order(mx_ref.matmul(q, mx_ref.quantize(w))[A::8])[:, :A]
            sent.append(mx_ref.quantize(np.concatenate([gcols(z, e), gcols(w, h)], axis=1)))
            pl.append(along(along(ol[r], a), e))
            pg.append(along(along(og[r], c), h))
        came = decode(join(*sent)).astype(BF)
        for r in range(N):
            i, j = (r - 1) % N, (r + 1) % N
            got = np.concatenate([cut(came, 2 * i, 4 * A), cut(came, 2 * j + 1, 4 * A)], axis=1)
            q = mx_ref.quantize(got)
            new = tile([np.maximum(mx_ref.matmul(pick(lay[r], np.arange(128 * b, 128 * b + 128)), q), np.float32(0.0)) * np.float32(0.03125) + got[:, b::4].astype(np.float32) for b in range(4)])
            left[r], right[r] = new[:, :4 * A], new[:, 4 * A:]
            ol[r], og[r] = pl[i], pg[j]
    y, ot = np.zeros((N, 128, 2 * A), np.float32), np.zeros((N, 8, 2 * A), np.float32)
    oc, osc = np.zeros((N, 128, 8 * A), np.uint8), np.zeros((N, 16, 2 * A), np.uint8)
    for r in range(N):
        q = mx_ref.quantize(np.concatenate([left[r], right[r]], axis=1))
        y[r] = mx_ref.matmul(mx_ref.quantize(v[r]), q)
        ot[r] = np.concatenate([ol[r], og[r]], axis=1)
        oc[r], osc[r] = emit(q)
    return {"y": y, "ot": ot, "oc": oc, "osc": osc}

@@ -1,0 +1,363 @@
+from concourse.bass import DstId, RemoteDMATransfer
+from concourse.mybir import dt, AluOpType, ActivationFunctionType
+
+N, C, A, R = 8, 320, 64, 3
+NS = (5, 0)
+ZAT = 8
+BIG = 2.0 ** 90
+
+SCRATCH = {}
+
+
+def sbuf(kind, **names):
+    for k, n in names.items():
+        SCRATCH[k] = ("sbuf", [128, n], kind)
+
+
+BF, F4, I4, U2, Q8, U1 = "bfloat16", "float32", "int32", "uint16", "float8_e4m3fn_x4", "uint8"
+sbuf(I4, li=80, lj=80, lk=80, pki=16, qi=4, qj=4, oi=64, oj=128)
+sbuf(U2, op=40, pk=16, ot0=80, ot1=80, ot2=80, ot3=80)
+sbuf(BF, xt=4 * C, lr=512, bt=512, ft=512, vt=512, et=2048, hb=C)
+sbuf(Q8, vq=128, eq=512, wq=512, sq=128, st=256, fq=128)
+sbuf(U1, vs=128, es=512, wp=512, sp=128, ss=256, fs=128)
+sbuf(F4, rb=512, yo=128, qf=4, r16=C, r4=A, i4=C, m16=C, mb=C, rst=C, h16=A, m4=A, h4=A, olf=128, olo=64, ohi=64, osm=64, of=128)
+SCRATCH["pd"] = ("psum", [128, 2048], F4)
+SCRATCH["pw"] = ("psum", [128, 2048], F4)
+for _f in "01":
+    sbuf(BF, **{"xg" + _f: 4 * C, "zt" + _f: 4 * C, "ee" + _f: C, "xx" + _f: C, "cm" + _f: 20 * C, "pl" + _f: 512})
+    sbuf(F4, **{"aa" + _f: 2 * C, "yy" + _f: C, "mk" + _f: C, "sc" + _f: C, "nt" + _f: 20, "rk" + _f: 20, "rr" + _f: 20,
+                "inv" + _f: C, "em" + _f: A, "en" + _f: A, "gm" + _f: A, "gn" + _f: A, "oz" + _f: C})
+    sbuf(U2, **{"ro" + _f: 20, "of4" + _f: 16, "eo" + _f: 4})
+    sbuf(Q8, **{"zq" + _f: C, "pc" + _f + "0": 128, "pc" + _f + "1": 128, "pc" + _f + "2": 128})
+    sbuf(U1, **{"zs" + _f: C, "pp" + _f + "0": 128, "pp" + _f + "1": 128, "pp" + _f + "2": 128})
+for _r in "012":
+    sbuf(Q8, **{"lc" + _r: 128})
+    sbuf(U1, **{"lp" + _r: 128})
+    sbuf(U2, **{"ou" + _r: 64, "on" + _r: 64})
+SEMAPHORES = ["sV", "sS", "sT", "sG", "ls", "dl", "d0", "dx", "dw", "dv", "dy", "do", "ar0", "ar1", "ar2", "ao0", "ao1", "ao2"]
+
+
+def rank_program(g, core, T, topo):
+    rank = T.rank_of(core)
+    if rank is None:
+        return
+    OP, AF = AluOpType, ActivationFunctionType
+    Q = {"V": g.vector, "S": g.scalar, "T": g.tensor, "G": g, "Y": g.sync}
+    cnt, seen, snap, lastw, readers, lastx = {}, {e: {} for e in Q}, {}, {}, {}, {}
+
+    def wait(e, k, n):
+        if seen[e].get(k, 0) >= n:
+            return
+        Q[e].wait_ge(T.sem[k], n)
+        seen[e][k] = n
+        for a, b in snap.get((k, n), {}).items():
+            if seen[e].get(a, 0) < b:
+                seen[e][a] = b
+
+    def need(e, rd, wr, ps=()):
+        own, want = "s" + e, {}
+        toks = [lastw[r] for r in list(rd) + list(wr) if r in lastw]
+        for w in wr:
+            toks += readers.get(w, [])
+        toks += [lastx[p] for p in ps if p in lastx and lastx[p][0] != own]
+        for k, n in toks:
+            n = cnt[k] if k[0] == "d" else n
+            want[k] = max(n, want.get(k, 0))
+        for k in sorted(want):
+            wait(e, k, want[k])
+
+    def note(tok, e, rd, wr, ps=()):
+        snap[tok] = dict(seen[e])
+        for r in rd:
+            readers.setdefault(r, []).append(tok)
+        for w in wr:
+            lastw[w], readers[w] = tok, []
+        for p in ps:
+            lastx[p] = tok
+
+    def op(e, f, rd, wr, ps=()):
+        need(e, rd, wr, ps)
+        k = "s" + e
+        cnt[k] = cnt.get(k, 0) + 1
+        f(Q[e]).then_inc(T.sem[k], 1)
+        note((k, cnt[k]), e, rd, wr, ps)
+
+    def tt(o, a, b, how, rd, wr, ps=()):
+        op("V", lambda q: q.tensor_tensor(o, a, b, how), rd, wr, ps)
+
+    def ts(o, a, s1, s2, o1, o2, rd, wr, ps=()):
+        if o2 is None:
+            op("V", lambda q: q.tensor_scalar(o, a, s1, None, o1), rd, wr, ps)
+        else:
+            op("V", lambda q: q.tensor_scalar(o, a, s1, s2, o1, o2), rd, wr, ps)
+
+    def tc(o, a, rd, wr, ps=()):
+        op("V", lambda q: q.tensor_copy(o, a), rd, wr, ps)
+
+    def scan(o, a, b, first, o1, o2, rd, wr):
+        op("V", lambda q: q.tensor_tensor_scan(o, a, b, first, o1, o2), rd, wr)
+
+    def quant(c, s, t, rd, wr):
+        op("V", lambda q: q.quantize_mx(c, s, t), rd, wr)
+
+    def act(o, i, func, rd, wr, ps=(), **kw):
+        op("S", lambda q: q.activation(o, i, func, **kw), rd, wr, ps)
+
+    def mm(bank, o, w, ws, x, xs, rd):
+        op("T", lambda q: q.matmul_mx(o, w, ws, x, xs, True, True), rd, [], [bank])
+
+    def dma(e, out, in_, rd, wr, k):
+        need(e, rd, wr)
+        cnt[k] = cnt.get(k, 0) + 16
+        Q[e].dma_start(out, in_).then_inc(T.sem[k], 16)
+        note((k, cnt[k]), e, rd, wr)
+
+    BT = ["bt0", "bt1", "bt2", "bt3", "bth"]
+
+    for i, nm in enumerate(("la", "lx", "ra", "rx")):
+        dma("S", T.li[:, 20 * i:20 * i + 20], T[nm][:, :], [], ["li%d" % i], "dl")
+    LI = ["li0", "li1", "li2", "li3"]
+    dma("Y", T.xt[:, :], T.x[:, :], [], ["xt"], "dx")
+    dma("Y", T.lr[:, 0:256], T.l0[:, :], [], ["lr0"], "d0")
+    dma("Y", T.lr[:, 256:512], T.r0[:, :], [], ["lr1"], "d0")
+    dma("Y", T.wq[:, :].bitcast(dt.uint8), T.wc[:, :], [], ["wq"], "dw")
+    dma("Y", T.wp[:, :], T.ws[:, :], [], ["wp"], "dw")
+    dma("Y", T.vt[:, :], T.v[:, :], [], ["vt"], "dv")
+
+    def iota(o, pattern, base, mult, wr, **kw):
+        op("G", lambda q: q.iota(o, pattern, base, mult, **kw), [], wr)
+    big = {"allow_small_or_imprecise_dtypes": True}
+    iota(T.qi[:, 3:4], [[1, 1]], 0, 1, ["qi"])
+    iota(T.pki[:, 0:8], [[8, 8]], 64, 0, ["pki"])
+    iota(T.pki[:, 8:16], [[8, 8]], 0, 0, ["pki2"])
+    iota(T.r16[:, :], [[0, 20], [1, 16]], 0, 0, ["r16"], **big)
+    iota(T.olf[:, :], [[32, 2], [0, 2], [1, 32]], 0, 0, ["olf"], **big)
+    iota(T.i4[:, :], [[4, C]], 0, 0, ["i4"], **big)
+    iota(T.r4[:, :], [[0, 16], [1, 4]], 0, 0, ["r4"], **big)
+    op("V", lambda q: q.memset(T.et[:, :], 0.0), [], ["et0", "et1", "et2", "et3"])
+    for b in range(4):
+        e = T.et[:, 512 * b:512 * b + 512]
+        op("G", lambda q: q.affine_select(e, e, [[1, 512]], OP.not_equal, 0.5, -b, -4), ["et%d" % b], ["et%d" % b])
+    tc(T.pk[:, :], T.pki[:, :], ["pki", "pki2"], ["pk"])
+    for f in range(2):
+        op("V", lambda q: q.memset(T["pl%d" % f][:, 256:512], 0.0), [], ["pz%d" % f])
+    for t in range(4):
+        ts(T["ot%d" % t][:, :], T.li[:, :], 4.0, float(t), OP.mult, OP.add, LI, ["ot%d" % t])
+    act(T.bt[:, 0:256], T.lr[:, 0:256], AF.Copy, ["lr0"], ["bth"], scale=0.5)
+    act(T.bt[:, 256:512], T.lr[:, 256:512], AF.Copy, ["lr1"], BT[:4], scale=0.5)
+
+    def xgather(e, f, t):
+        o = T["xg%d" % f][:, C * t:C * t + C]
+        w = T.xt[:, :].indirect(T["ot%d" % t][:, 40 * f + 20:40 * f + 40])
+        if e == "S":
+            act(o, w, AF.Copy, ["xt", "ot%d" % t], ["xg%d%d" % (f, t)], scale=0.5)
+        else:
+            ts(o, w, 0.5, None, OP.mult, None, ["xt", "ot%d" % t], ["xg%d%d" % (f, t)])
+
+    def constants():
+        ts(T.qj[:, 0:1], T.qi[:, 3:4], 15, None, OP.bitwise_and, None, ["qi"], ["qj0"])
+        ts(T.qj[:, 1:2], T.qi[:, 3:4], 2, 3, OP.logical_shift_right, OP.bitwise_and, ["qi"], ["qj1"])
+        ts(T.qj[:, 2:3], T.qi[:, 3:4], 3, None, OP.bitwise_and, None, ["qi"], ["qj2"])
+        tc(T.qf[:, 0:3], T.qj[:, 0:3], ["qj0", "qj1", "qj2"], ["qf"])
+        ts(T.m16[:, :], T.r16[:, :], T.qf[:, 0:1], None, OP.is_equal, None, ["r16", "qf"], ["m16"])
+        ts(T.rst[:, :], T.r16[:, :], 0.0, 2 * BIG, OP.is_gt, OP.mult, ["r16"], ["rst"])
+        ts(T.mb[:, :], T.m16[:, :], 2 * BIG, -BIG, OP.mult, OP.add, ["m16"], ["mb"])
+        ts(T.rst[:, :], T.rst[:, :], -BIG, None, OP.add, None, ["rst"], ["rst"])
+        ts(T.hb[:, :], T.r16[:, :], 0.0, None, OP.is_gt, None, ["r16"], ["hb"])
+        ts(T.h16[:, :], T.r16[:, 0:A], 0.0, None, OP.is_gt, None, ["r16"], ["h16"])
+        ts(T.h4[:, :], T.r4[:, :], 0.0, None, OP.is_gt, None, ["r4"], ["h4"])
+        ts(T.m4[:, :], T.r4[:, :], T.qf[:, 1:2], None, OP.is_equal, None, ["r4", "qf"], ["m4"])
+        ts(T.lj[:, :], T.li[:, :], 32.0, 32.0, OP.is_ge, OP.mult, LI, ["lj"])
+        tt(T.lk[:, :], T.lj[:, :], T.li[:, :], OP.add, ["lj"] + LI, ["lk"])
+        tc(T.op[:, 0:20], T.lk[:, 0:20], ["lk"], ["op0"])
+        ts(T.op[:, 20:40], T.lk[:, 40:60], 32.0, None, OP.add, None, ["lk"], ["op1"])
+
+    def stationary():
+        quant(T.sq[:, :], T.sp[:, :], T.bt[:, :], BT, ["sq"])
+        tc(T.st[:, 0:256].bitcast(dt.uint32), T.sq[:, 0:128].bitcast(dt.uint32).indirect(T.pk[:, 0:16]), ["sq", "pk"], ["st"])
+        act(T.ss[:, 0:256], T.sp[:, 0:128].indirect(T.pk[:, 0:16]), AF.Copy, ["sq", "pk"], ["ss"])
+
+    def cand(f, t):
+        w = T.bt[:, 256 * f:256 * f + 256].indirect(T["ot%d" % t][:, 40 * f:40 * f + 20])
+        tt(T["zt%d" % f][:, t:4 * C:4], w, T["xg%d" % f][:, C * t:C * t + C], OP.add, BT + ["ot%d" % t, "xg%d%d" % (f, t)], ["zt%d%d" % (f, t)])
+
+    def score(f):
+        u = "%d" % f
+        quant(T["zq" + u][:, :], T["zs" + u][:, :], T["zt" + u][:, :], ["zt" + u + "%d" % t for t in range(4)], ["zq" + u])
+        s, k = slice(128 * f, 128 * f + 128), T.pw[:, 512 * f:512 * f + C]
+        mm("pw" + u, k, T.st[:, s], T.ss[:, s], T["zq" + u][:, :], T["zs" + u][:, :], ["st", "ss", "zq" + u])
+        act(T["aa" + u][:, C:2 * C], k, AF.Copy, [], ["ap" + u], ["pw" + u])
+        act(T["yy" + u][:, :], T["aa" + u][:, C:2 * C], AF.Abs, ["ap" + u], ["yy" + u], bias=2.0 ** -125, scale=0.6 * 2.0 ** -23)
+
+    def prep(f):
+        u = "%d" % f
+        k = T.pw[:, 512 * f:512 * f + C]
+        tt(T["mk" + u][:, :], k, T.mb[:, :], OP.min, ["mb"], ["mk" + u], ["pw" + u])
+        scan(T["sc" + u][:, :], T.rst[:, :], T["mk" + u][:, :], -BIG, OP.min, OP.max, ["rst", "mk" + u], ["sc" + u])
+        tt(T["aa" + u][:, 0:C], k, T["yy" + u][:, :], OP.subtract, ["yy" + u], ["am" + u], ["pw" + u])
+        if NS[f]:
+            act(T["nt" + u][:, :], T["sc" + u][:, 15:C:16], AF.Copy, ["sc" + u], ["nt" + u], scale=-1.0)
+
+    def ties(f):
+        u = "%d" % f
+        tt(T["ee" + u][:, :], T.pw[:, 512 * f:512 * f + C], T["sc" + u][:, :], OP.is_equal, ["sc" + u], ["ee" + u], ["pw" + u])
+        scan(T["xx" + u][:, :], T.hb[:, :], T["ee" + u][:, :], 0.0, OP.mult, OP.add, ["hb", "ee" + u], ["xx" + u])
+
+    def slot(f, c):
+        return T["cm%d" % f][:, C * c:C * c + C], ["cm%d%d" % (f, c)], ["rk%d%d" % (f, c)], T["aa%d" % f][:, 16 * c + 16:16 * c + 16 + C], T["rk%d" % f][:, c:c + 1]
+
+    def alone(f, c):
+        m, cm, rk, w, o = slot(f, c)
+        act(m, w, AF.Sign, ["ap%d" % f, "am%d" % f, "nt%d" % f], cm, bias=T["nt%d" % f][:, c:c + 1])
+        act(m, m, AF.Sign, cm, cm + rk, bias=0.5, accum_out=o)
+
+    def compare(f, c):
+        m, cm, rk, w, o = slot(f, c)
+        ts(m, w, T["sc%d" % f][:, 16 * c + 15:16 * c + 16], None, OP.is_ge, None, ["ap%d" % f, "am%d" % f, "sc%d" % f], cm)
+        act(m, m, AF.Copy, cm, cm + rk, accum_out=o)
+
+    def survive(f, r):
+        u = "%d" % f
+        n = "%d%d" % (f, r)
+        tt(T["rr" + u][:, :], T["rk" + u][:, :], T["xx" + u][:, 15:C:16], OP.subtract, ["rk%d%d" % (f, c) for c in range(20)] + ["xx" + u], ["rr" + u])
+        tc(T["ro" + u][:, :], T["rr" + u][:, :], ["rr" + u], ["ro" + u])
+        tc(T["inv" + u][:, :].indirect(T["ro" + u][:, 0:20]), T.i4[:, :], ["ro" + u, "i4"], ["inv" + u])
+        tt(T["gm" + u][:, :], T["inv" + u][:, 0:A], T.m4[:, :], OP.mult, ["inv" + u, "m4"], ["gm" + u])
+        scan(T["gn" + u][:, :], T.h4[:, :], T["gm" + u][:, :], 0.0, OP.mult, OP.add, ["gm" + u, "h4"], ["gn" + u])
+        ts(T["of4" + u][:, :], T["gn" + u][:, 3:A:4], T.qf[:, 2:3], None, OP.add, None, ["gn" + u, "qf"], ["of4" + u])
+        tc(T["pl" + u][:, 0:256], T["zt" + u][:, :].indirect(T["of4" + u][:, 0:16]), ["of4" + u] + ["zt" + u + "%d" % t for t in range(4)], ["pl" + u])
+        quant(T["pc" + n][:, :], T["pp" + n][:, :], T["pl" + u][:, :], ["pl" + u, "pz" + u], ["pc" + n])
+        d = T.cores[(rank + 1 - 2 * f) % N]
+        rid, pid = topo.addr(d, core)
+        m, ne = topo.mask(core, d), len(topo.engines(core, d))
+        s, k = slice(64 * f, 64 * f + 64), "ar%d" % r
+        need("G", ["pc" + n], [])
+        g.remote_dma(T["lc%d" % r][:, s].bitcast(dt.uint8), T["pc" + n][:, 0:64].bitcast(dt.uint8), T.sem[k], T.sem.ls, pid, rid, m)
+        g.remote_dma(T["lp%d" % r][:, s], T["pp" + n][:, 0:64], T.sem[k], T.sem.ls, pid, rid, m)
+        cnt["ls"] = cnt.get("ls", 0) + 2 * ne
+        cnt[k] = cnt.get(k, 0) + 2 * ne
+
+    def etable(f):
+        u = "%d" % f
+        tt(T["em" + u][:, :], T["inv" + u][:, 0:A], T.m16[:, 0:A], OP.mult, ["inv" + u, "m16"], ["em" + u])
+        scan(T["en" + u][:, :], T.h16[:, :], T["em" + u][:, :], 0.0, OP.mult, OP.add, ["em" + u, "h16"], ["en" + u])
+        ts(T["eo" + u][:, :], T["en" + u][:, 15:A:16], 0.25, None, OP.mult, None, ["en" + u], ["eo" + u])
+        s = slice(32 * f, 32 * f + 32)
+        act(T.olo[:, s], T["oz" + u][:, :].indirect(T["eo" + u][:, 0:2]), AF.Copy, ["oz" + u, "eo" + u], ["olo" + u])
+        act(T.ohi[:, s], T["oz" + u][:, :].indirect(T["eo" + u][:, 2:4]), AF.Copy, ["oz" + u, "eo" + u], ["ohi" + u], scale=64.0)
+
+    def origins_out(r):
+        n = "%d" % r
+        tt(T.osm[:, :], T.olo[:, :], T.ohi[:, :], OP.add, ["olo0", "olo1", "ohi0", "ohi1"], ["osm"])
+        tc(T["ou" + n][:, :], T.osm[:, :], ["osm"], ["ou" + n])
+        need("G", ["ou" + n], [])
+        tr = []
+        for f in range(2):
+            d = T.cores[(rank + 1 - 2 * f) % N]
+            rid, pid = topo.addr(d, core)
+            en = topo.engines(core, d)
+            h, s = len(en) // 2, slice(32 * f, 32 * f + 32)
+            tr.append(RemoteDMATransfer(dst_ids=[DstId(rid=rid, pnc=pid)], dma_engine_mask=sum(1 << e for e in en[h * f:h * f + h]),
+                                        remote_sem=T.sem["ao" + n], src=T["ou" + n][:, s], dst=T["on" + n][:, s]))
+            cnt["ls"] += h
+            cnt["ao" + n] = cnt.get("ao" + n, 0) + h
+        g.remote_dma_fused(tr, local_sem=T.sem.ls)
+
+    def origins_in(r, last):
+        n = "%d" % r
+        lastw["on" + n] = ("ao" + n, cnt["ao" + n])
+        tc(T.oi[:, :], T["on" + n][:, :], ["on" + n], ["oi"])
+        ts(T.oj[:, 0:64], T.oi[:, :], 63, None, OP.bitwise_and, None, ["oi"], ["oj0"])
+        ts(T.oj[:, 64:128], T.oi[:, :], 6, None, OP.logical_shift_right, None, ["oi"], ["oj1"])
+        if not last:
+            tc(T.olf[:, :], T.oj[:, :], ["oj0", "oj1"], ["olf"])
+            return
+        for f in range(2):
+            base = float(A * ((rank - R + 2 * R * f) % N))
+            for h in range(2):
+                o, i = 64 * f + 32 * h, 64 * h + 32 * f
+                ts(T.of[:, o:o + 32], T.oj[:, i:i + 32], base, None, OP.add, None, ["oj%d" % h], ["of%d%d" % (f, h)])
+        dma("Y", T.ot[:, :], T.of[0:128:16, :], ["of00", "of01", "of10", "of11"], [], "do")
+
+    def renew(r):
+        last = r == R - 1
+        n = "%d" % r
+        lastw["lc" + n] = ("ar" + n, cnt["ar" + n])
+        W = [slice(128 * b, 128 * b + 128) for b in range(4)]
+        P = [slice(512 * b, 512 * b + 128) for b in range(4)]
+        two = 2.0 if last else 1.0
+        for b in range(4):
+            mm("pd%d" % b, T.pd[:, P[b]], T.eq[:, W[b]], T.es[:, W[b]], T["lc" + n][:, :], T["lp" + n][:, :], ["lc" + n, "eq"])
+        for b in range(4):
+            o, i = T.ft[:, b:512:4], T.pd[:, P[b]]
+            if b % 2:
+                act(o, i, AF.Copy, [], ["ft%d" % b], ["pd%d" % b], scale=two)
+            else:
+                ts(o, i, two, None, OP.mult, None, [], ["ft%d" % b], ["pd%d" % b])
+        quant(T.fq[:, :], T.fs[:, :], T.ft[:, :], ["ft%d" % b for b in range(4)], ["fq"])
+        for b in range(4):
+            mm("pw%d" % b, T.pw[:, P[b]], T.wq[:, W[b]], T.wp[:, W[b]], T.fq[:, :], T.fs[:, :], ["wq", "wp", "fq"])
+        for b in range(4):
+            act(T.rb[:, W[b]], T.pw[:, P[b]], AF.Relu, [], ["rb%d" % b], ["pw%d" % b], scale=0.03125)
+        for b in range(4):
+            o = T.bt[:, b:512:4]
+            if last:
+                tt(o, T.rb[:, W[b]], T.ft[:, b:512:4], OP.add, ["rb%d" % b, "ft%d" % b], ["bt%d" % b])
+            else:
+                tt(o, T.rb[:, W[b]], T.pd[:, P[b]], OP.add, ["rb%d" % b], ["bt%d" % b], ["pd%d" % b])
+
+    for r in range(R):
+        if r == 0:
+            constants()
+            for t in range(4):
+                xgather("S" if t < 2 else "V", 0, t)
+        stationary()
+        for t in range(4):
+            cand(0, t)
+        score(0)
+        if r == 0:
+            for t in range(4):
+                xgather("S" if t < 2 else "V", 1, t)
+        cand(1, 0)
+        cand(1, 1)
+        prep(0)
+        cand(1, 2)
+        cand(1, 3)
+        for c in range(NS[0]):
+            alone(0, c)
+        score(1)
+        ties(0)
+        if r:
+            origins_in(r - 1, False)
+        for f in range(2):
+            act(T["oz%d" % f][:, :], T.olf[:, :].indirect(T.op[:, 20 * f:20 * f + 20]), AF.Copy, ["olf", "op%d" % f], ["oz%d" % f])
+        if NS[0]:
+            names = ["rk0%d" % c for c in range(NS[0])]
+            act(T.rk0[:, 0:NS[0]], T.rk0[:, 0:NS[0]], AF.Copy, names, names, bias=C / 2.0, scale=0.5)
+        for c in range(NS[0], 20):
+            compare(0, c)
+        prep(1)
+        ties(1)
+        for c in range(20):
+            if c == ZAT:
+                survive(0, r)
+            compare(1, c)
+        if r == 0:
+            quant(T.eq[:, :], T.es[:, :], T.et[:, :], ["et%d" % b for b in range(4)], ["eq"])
+            quant(T.vq[:, :], T.vs[:, :], T.vt[:, :], ["vt"], ["vq"])
+        survive(1, r)
+        etable(0)
+        etable(1)
+        origins_out(r)
+        renew(r)
+
+    quant(T.sq[:, :], T.sp[:, :], T.bt[:, :], BT, ["sq"])
+    dma("Y", T.oc[:, :], T.sq[:, :].bitcast(dt.uint8), ["sq"], [], "do")
+    mm("pw0", T.pw[:, 0:128], T.vq[:, :], T.vs[:, :], T.sq[:, :], T.sp[:, :], ["vq", "sq"])
+    act(T.yo[:, :], T.pw[:, 0:128], AF.Copy, [], ["yo"], ["pw0"])
+    dma("S", T.y[:, :], T.yo[:, :], ["yo"], [], "dy")
+    for k in range(4):
+        dma("Y", T.osc[4 * k:4 * k + 4, :], T.sp[32 * k:32 * k + 4, :], ["sq"], [], "do")
+    origins_in(R - 1, True)
+    for k in sorted(cnt):
+        wait("G", k, cnt[k])

@@ -2,9 +2,15 @@ from concourse.bass import DstId, RemoteDMATransfer
 from concourse.mybir import dt, AluOpType, ActivationFunctionType
 
 N, C, A, R = 8, 320, 64, 3
-NS = (5, 0)
-ZAT = 8
 BIG = 2.0 ** 90
+TILES = [[19, 18, 17], [16, 15, 14, 13], [12, 11, 10, 9], [8, 7, 6, 5], [4, 3, 2, 1], [0]]
+WIDE = [C, 272, 208, 144, 128, 128]
+AT = [sum(WIDE[:j]) for j in range(7)]
+LAST = 2
+ALONE = TILES[0] + TILES[LAST]
+REST = [j for j in range(1, 6) if j != LAST]
+OWN = [c for j in REST for c in TILES[j]]
+WHERE = {c: (j, t) for j in range(6) for t, c in enumerate(TILES[j])}
 
 SCRATCH = {}
 
@@ -16,25 +22,22 @@ def sbuf(kind, **names):
 
 BF, F4, I4, U2, Q8, U1 = "bfloat16", "float32", "int32", "uint16", "float8_e4m3fn_x4", "uint8"
 sbuf(I4, li=80, lj=80, lk=80, pki=16, qi=4, qj=4, oi=64, oj=128)
-sbuf(U2, op=40, pk=16, ot0=80, ot1=80, ot2=80, ot3=80)
-sbuf(BF, xt=4 * C, lr=512, bt=512, ft=512, vt=512, et=2048, hb=C)
-sbuf(Q8, vq=128, eq=512, wq=512, sq=128, st=256, fq=128)
-sbuf(U1, vs=128, es=512, wp=512, sp=128, ss=256, fs=128)
-sbuf(F4, rb=512, yo=128, qf=4, r16=C, r4=A, i4=C, m16=C, mb=C, rst=C, h16=A, m4=A, h4=A, olf=128, olo=64, ohi=64, osm=64, of=128)
+sbuf(U2, op=40, pk=16, off=320, ou=64 * R, on=64 * R)
+sbuf(BF, xt=4 * C, lr=512, bt=512, vt=512, et=2048, aw=1536, i8=512, zz=512, jk=4 * C, sg=4 * C)
+sbuf(Q8, vq=128, eq=512, aq=384, zc=128, wq=512, sq=128, st=256)
+sbuf(U1, vs=128, es=512, ax=384, zp=128, wp=512, sp=128, ss=256)
+sbuf(F4, rb=512, yo=128, qf=4, r16=C, r4=A, i4=C, m16=C, mb=C, rst=C, h16=C, m4=A, h4=A, olf=128, olo=64, ohi=64, osm=64, of=128, cc=20)
 SCRATCH["pd"] = ("psum", [128, 2048], F4)
 SCRATCH["pw"] = ("psum", [128, 2048], F4)
 for _f in "01":
-    sbuf(BF, **{"xg" + _f: 4 * C, "zt" + _f: 4 * C, "ee" + _f: C, "xx" + _f: C, "cm" + _f: 20 * C, "pl" + _f: 512})
-    sbuf(F4, **{"aa" + _f: 2 * C, "yy" + _f: C, "mk" + _f: C, "sc" + _f: C, "nt" + _f: 20, "rk" + _f: 20, "rr" + _f: 20,
+    sbuf(BF, **{"xg" + _f: 4 * C, "zt" + _f: 4 * C, "pl" + _f: 512, "ft" + _f: 512, "ut" + _f: 4 * AT[6]})
+    sbuf(F4, **{"ap" + _f: C, "mk" + _f: C, "sc" + _f: C, "nt" + _f: 20, "rk" + _f: 20, "rr" + _f: 20, "rs" + _f: 20, "md" + _f: C, "dd" + _f: C,
                 "inv" + _f: C, "em" + _f: A, "en" + _f: A, "gm" + _f: A, "gn" + _f: A, "oz" + _f: C})
     sbuf(U2, **{"ro" + _f: 20, "of4" + _f: 16, "eo" + _f: 4})
-    sbuf(Q8, **{"zq" + _f: C, "pc" + _f + "0": 128, "pc" + _f + "1": 128, "pc" + _f + "2": 128})
-    sbuf(U1, **{"zs" + _f: C, "pp" + _f + "0": 128, "pp" + _f + "1": 128, "pp" + _f + "2": 128})
-for _r in "012":
-    sbuf(Q8, **{"lc" + _r: 128})
-    sbuf(U1, **{"lp" + _r: 128})
-    sbuf(U2, **{"ou" + _r: 64, "on" + _r: 64})
-SEMAPHORES = ["sV", "sS", "sT", "sG", "ls", "dl", "d0", "dx", "dw", "dv", "dy", "do", "ar0", "ar1", "ar2", "ao0", "ao1", "ao2"]
+    sbuf(Q8, **{"zq" + _f: C, "uq" + _f: AT[6], "fq" + _f: 128, "pc" + _f: 128 * R, "lc" + _f: 256})
+    sbuf(U1, **{"zs" + _f: C, "us" + _f: AT[6], "fs" + _f: 128, "pp" + _f: 128 * R, "lp" + _f: 256})
+SEMAPHORES = ["sV", "sS", "sT", "sG", "ls", "dl", "d0", "dx", "dw", "dv", "dz", "dy", "do", "ao0", "ao1", "ao2"]
+SEMAPHORES += ["ar%d%d" % (_f, _r) for _f in range(2) for _r in range(R)]
 
 
 def rank_program(g, core, T, topo):
@@ -43,7 +46,7 @@ def rank_program(g, core, T, topo):
         return
     OP, AF = AluOpType, ActivationFunctionType
     Q = {"V": g.vector, "S": g.scalar, "T": g.tensor, "G": g, "Y": g.sync}
-    cnt, seen, snap, lastw, readers, lastx = {}, {e: {} for e in Q}, {}, {}, {}, {}
+    cnt, seen, snap, lastw, readers, lastx = {"ls": 0}, {e: {} for e in Q}, {}, {}, {}, {}
 
     def wait(e, k, n):
         if seen[e].get(k, 0) >= n:
@@ -94,6 +97,9 @@ def rank_program(g, core, T, topo):
     def tc(o, a, rd, wr, ps=()):
         op("V", lambda q: q.tensor_copy(o, a), rd, wr, ps)
 
+    def fill(o, v, wr):
+        op("V", lambda q: q.memset(o, v), [], wr)
+
     def scan(o, a, b, first, o1, o2, rd, wr):
         op("V", lambda q: q.tensor_tensor_scan(o, a, b, first, o1, o2), rd, wr)
 
@@ -103,8 +109,8 @@ def rank_program(g, core, T, topo):
     def act(o, i, func, rd, wr, ps=(), **kw):
         op("S", lambda q: q.activation(o, i, func, **kw), rd, wr, ps)
 
-    def mm(bank, o, w, ws, x, xs, rd):
-        op("T", lambda q: q.matmul_mx(o, w, ws, x, xs, True, True), rd, [], [bank])
+    def mm(bank, o, w, ws, x, xs, rd, start=True, stop=True):
+        op("T", lambda q: q.matmul_mx(o, w, ws, x, xs, start, stop), rd, [], [bank])
 
     def dma(e, out, in_, rd, wr, k):
         need(e, rd, wr)
@@ -112,43 +118,77 @@ def rank_program(g, core, T, topo):
         Q[e].dma_start(out, in_).then_inc(T.sem[k], 16)
         note((k, cnt[k]), e, rd, wr)
 
-    BT = ["bt0", "bt1", "bt2", "bt3", "bth"]
+    def iota(o, pattern, base, mult, wr, **kw):
+        op("G", lambda q: q.iota(o, pattern, base, mult, **kw), [], wr)
+
+    def run(*gens):
+        gens = list(gens)
+        while gens:
+            for x in list(gens):
+                if next(x, 1) is not None:
+                    gens.remove(x)
+
+    def chain(*gens):
+        for x in gens:
+            yield from x
+
+    HALF = [["b%d%d" % (h, b) for b in range(4)] for h in range(2)]
+    LI = ["li0", "li1", "li2", "li3"]
 
     for i, nm in enumerate(("la", "lx", "ra", "rx")):
-        dma("S", T.li[:, 20 * i:20 * i + 20], T[nm][:, :], [], ["li%d" % i], "dl")
-    LI = ["li0", "li1", "li2", "li3"]
-    dma("Y", T.xt[:, :], T.x[:, :], [], ["xt"], "dx")
+        dma("S", T.li[:, 20 * i:20 * i + 20], T[nm][:, :], [], [LI[i]], "dl")
     dma("Y", T.lr[:, 0:256], T.l0[:, :], [], ["lr0"], "d0")
     dma("Y", T.lr[:, 256:512], T.r0[:, :], [], ["lr1"], "d0")
+    dma("Y", T.xt[:, :], T.x[:, :], [], ["xt"], "dx")
     dma("Y", T.wq[:, :].bitcast(dt.uint8), T.wc[:, :], [], ["wq"], "dw")
     dma("Y", T.wp[:, :], T.ws[:, :], [], ["wp"], "dw")
     dma("Y", T.vt[:, :], T.v[:, :], [], ["vt"], "dv")
 
-    def iota(o, pattern, base, mult, wr, **kw):
-        op("G", lambda q: q.iota(o, pattern, base, mult, **kw), [], wr)
     big = {"allow_small_or_imprecise_dtypes": True}
     iota(T.qi[:, 3:4], [[1, 1]], 0, 1, ["qi"])
     iota(T.pki[:, 0:8], [[8, 8]], 64, 0, ["pki"])
     iota(T.pki[:, 8:16], [[8, 8]], 0, 0, ["pki2"])
     iota(T.r16[:, :], [[0, 20], [1, 16]], 0, 0, ["r16"], **big)
-    iota(T.olf[:, :], [[32, 2], [0, 2], [1, 32]], 0, 0, ["olf"], **big)
-    iota(T.i4[:, :], [[4, C]], 0, 0, ["i4"], **big)
     iota(T.r4[:, :], [[0, 16], [1, 4]], 0, 0, ["r4"], **big)
-    op("V", lambda q: q.memset(T.et[:, :], 0.0), [], ["et0", "et1", "et2", "et3"])
+    iota(T.i8[:, :], [[1, 8], [0, 64]], 0, 0, ["i8"], **big)
+    val = [2 * (16 * (20 - c) - 1 - 8 * sum(a >= c for a in ALONE)) + (16 * c if c in ALONE else 0) for c in range(20)]
+    runs, c = [], 0
+    while c < 20:
+        d, e = (val[c + 1] - val[c] if c < 19 else 0), c + 1
+        while e < 20 and val[e] - val[e - 1] == d:
+            e += 1
+        runs.append("cc%d" % c)
+        iota(T.cc[:, c:e], [[d, e - c]], val[c], 0, [runs[-1]], **big)
+        c = e
+    iota(T.i4[:, :], [[4, C]], 0, 0, ["i4"], **big)
+    iota(T.olf[:, :], [[32, 2], [0, 2], [1, 32]], 0, 0, ["olf"], **big)
+    fill(T.zz[:, :], 0.0, ["zz"])
     for b in range(4):
         e = T.et[:, 512 * b:512 * b + 512]
-        op("G", lambda q: q.affine_select(e, e, [[1, 512]], OP.not_equal, 0.5, -b, -4), ["et%d" % b], ["et%d" % b])
+        op("G", lambda q: q.affine_select(e, T.zz[:, :], [[1, 512]], OP.not_equal, 0.5, -b, -4), ["zz"], ["et%d" % b])
+    quant(T.zc[:, :], T.zp[:, :], T.zz[:, :], ["zz"], ["zc"])
+    for f in range(2):
+        u = "%d" % f
+        dma("Y", T["lc" + u][:, 0:64].bitcast(dt.uint8), T.zc[:, 0:64].bitcast(dt.uint8), ["zc"], ["pad" + u], "dz")
+        dma("Y", T["lp" + u][:, 0:64], T.zp[:, 0:64], ["zc"], ["pae" + u], "dz")
     tc(T.pk[:, :], T.pki[:, :], ["pki", "pki2"], ["pk"])
     for f in range(2):
-        op("V", lambda q: q.memset(T["pl%d" % f][:, 256:512], 0.0), [], ["pz%d" % f])
+        u = "%d" % f
+        for j in range(6):
+            z = T["ut" + u][:, 4 * (AT[j] + (16 * (TILES[j][-1] + 1) if j < 5 else 0)):4 * AT[j + 1]]
+            fill(z, 0.0, ["u%d%d%d" % (f, j, t) for t in range(4)])
+        fill(T["pl" + u][:, 256:512], 0.0, ["pz" + u])
+        fill(T["ft" + u][:, 256:512], 0.0, ["fz" + u])
+        fill(T["rk" + u][:, 0:1], 0.0, ["rk%s0" % u])
+
     for t in range(4):
-        ts(T["ot%d" % t][:, :], T.li[:, :], 4.0, float(t), OP.mult, OP.add, LI, ["ot%d" % t])
-    act(T.bt[:, 0:256], T.lr[:, 0:256], AF.Copy, ["lr0"], ["bth"], scale=0.5)
-    act(T.bt[:, 256:512], T.lr[:, 256:512], AF.Copy, ["lr1"], BT[:4], scale=0.5)
+        ts(T.off[:, 80 * t:80 * t + 80], T.li[:, :], 4.0, float(t), OP.mult, OP.add, LI, ["ot%d" % t])
+    act(T.bt[:, 0:256], T.lr[:, 0:256], AF.Copy, ["lr0"], HALF[0], scale=0.5)
+    act(T.bt[:, 256:512], T.lr[:, 256:512], AF.Copy, ["lr1"], HALF[1], scale=0.5)
 
     def xgather(e, f, t):
         o = T["xg%d" % f][:, C * t:C * t + C]
-        w = T.xt[:, :].indirect(T["ot%d" % t][:, 40 * f + 20:40 * f + 40])
+        w = T.xt[:, :].indirect(T.off[:, 80 * t + 40 * f + 20:80 * t + 40 * f + 40])
         if e == "S":
             act(o, w, AF.Copy, ["xt", "ot%d" % t], ["xg%d%d" % (f, t)], scale=0.5)
         else:
@@ -158,117 +198,193 @@ def rank_program(g, core, T, topo):
         ts(T.qj[:, 0:1], T.qi[:, 3:4], 15, None, OP.bitwise_and, None, ["qi"], ["qj0"])
         ts(T.qj[:, 1:2], T.qi[:, 3:4], 2, 3, OP.logical_shift_right, OP.bitwise_and, ["qi"], ["qj1"])
         ts(T.qj[:, 2:3], T.qi[:, 3:4], 3, None, OP.bitwise_and, None, ["qi"], ["qj2"])
-        tc(T.qf[:, 0:3], T.qj[:, 0:3], ["qj0", "qj1", "qj2"], ["qf"])
+        ts(T.qj[:, 3:4], T.qi[:, 3:4], 4, None, OP.logical_shift_right, None, ["qi"], ["qj3"])
+        tc(T.qf[:, :], T.qj[:, :], ["qj0", "qj1", "qj2", "qj3"], ["qf"])
         ts(T.m16[:, :], T.r16[:, :], T.qf[:, 0:1], None, OP.is_equal, None, ["r16", "qf"], ["m16"])
-        ts(T.rst[:, :], T.r16[:, :], 0.0, 2 * BIG, OP.is_gt, OP.mult, ["r16"], ["rst"])
+        ts(T.h16[:, :], T.r16[:, :], 0.0, None, OP.is_gt, None, ["r16"], ["h16"])
         ts(T.mb[:, :], T.m16[:, :], 2 * BIG, -BIG, OP.mult, OP.add, ["m16"], ["mb"])
-        ts(T.rst[:, :], T.rst[:, :], -BIG, None, OP.add, None, ["rst"], ["rst"])
-        ts(T.hb[:, :], T.r16[:, :], 0.0, None, OP.is_gt, None, ["r16"], ["hb"])
-        ts(T.h16[:, :], T.r16[:, 0:A], 0.0, None, OP.is_gt, None, ["r16"], ["h16"])
+        ts(T.rst[:, :], T.h16[:, :], 2 * BIG, -BIG, OP.mult, OP.add, ["h16"], ["rst"])
         ts(T.h4[:, :], T.r4[:, :], 0.0, None, OP.is_gt, None, ["r4"], ["h4"])
         ts(T.m4[:, :], T.r4[:, :], T.qf[:, 1:2], None, OP.is_equal, None, ["r4", "qf"], ["m4"])
+        ts(T.aw[:, 512:1024], T.i8[:, :], T.qf[:, 3:4], -2.0, OP.is_equal, OP.mult, ["i8", "qf"], ["aw1"])
+
+    def constants2():
+        act(T.aw[:, 0:512], T.aw[:, 512:1024], AF.Copy, ["aw1"], ["aw0"], scale=0.5)
+        act(T.aw[:, 3:512:4], T.aw[:, 515:1024:4], AF.Copy, ["aw1"], ["aw0"], scale=-1.0)
+        act(T.aw[:, 1024:1536], T.aw[:, 512:1024], AF.Copy, ["aw1"], ["aw2"], scale=0.5)
+
+    def constants3():
+        quant(T.aq[:, :], T.ax[:, :], T.aw[:, :], ["aw0", "aw1", "aw2"], ["aq"])
+        yield
         ts(T.lj[:, :], T.li[:, :], 32.0, 32.0, OP.is_ge, OP.mult, LI, ["lj"])
+        yield
         tt(T.lk[:, :], T.lj[:, :], T.li[:, :], OP.add, ["lj"] + LI, ["lk"])
+        yield
         tc(T.op[:, 0:20], T.lk[:, 0:20], ["lk"], ["op0"])
         ts(T.op[:, 20:40], T.lk[:, 40:60], 32.0, None, OP.add, None, ["lk"], ["op1"])
 
-    def stationary():
-        quant(T.sq[:, :], T.sp[:, :], T.bt[:, :], BT, ["sq"])
-        tc(T.st[:, 0:256].bitcast(dt.uint32), T.sq[:, 0:128].bitcast(dt.uint32).indirect(T.pk[:, 0:16]), ["sq", "pk"], ["st"])
-        act(T.ss[:, 0:256], T.sp[:, 0:128].indirect(T.pk[:, 0:16]), AF.Copy, ["sq", "pk"], ["ss"])
+    def picks(f):
+        s, k = slice(128 * f, 128 * f + 128), T.pk[:, 8 * f:8 * f + 8]
+        tc(T.st[:, s].bitcast(dt.uint32), T.sq[:, 0:128].bitcast(dt.uint32).indirect(k), ["sq", "pk"], ["st%d" % f])
+        act(T.ss[:, s], T.sp[:, 0:128].indirect(k), AF.Copy, ["sq", "pk"], ["ss%d" % f])
 
-    def cand(f, t):
-        w = T.bt[:, 256 * f:256 * f + 256].indirect(T["ot%d" % t][:, 40 * f:40 * f + 20])
-        tt(T["zt%d" % f][:, t:4 * C:4], w, T["xg%d" % f][:, C * t:C * t + C], OP.add, BT + ["ot%d" % t, "xg%d%d" % (f, t)], ["zt%d%d" % (f, t)])
+    def cand(f, quarters):
+        for t in quarters:
+            w = T.bt[:, 256 * f:256 * f + 256].indirect(T.off[:, 80 * t + 40 * f:80 * t + 40 * f + 20])
+            tt(T["zt%d" % f][:, t:4 * C:4], w, T["xg%d" % f][:, C * t:C * t + C], OP.add, HALF[f] + ["ot%d" % t, "xg%d%d" % (f, t)], ["zt%d%d" % (f, t)])
+            yield
+
+    def zquant(f):
+        u = "%d" % f
+        quant(T["zq" + u][:, :], T["zs" + u][:, :], T["zt" + u][:, :], ["zt" + u + "%d" % t for t in range(4)], ["zq" + u])
+        yield
 
     def score(f):
         u = "%d" % f
-        quant(T["zq" + u][:, :], T["zs" + u][:, :], T["zt" + u][:, :], ["zt" + u + "%d" % t for t in range(4)], ["zq" + u])
         s, k = slice(128 * f, 128 * f + 128), T.pw[:, 512 * f:512 * f + C]
-        mm("pw" + u, k, T.st[:, s], T.ss[:, s], T["zq" + u][:, :], T["zs" + u][:, :], ["st", "ss", "zq" + u])
-        act(T["aa" + u][:, C:2 * C], k, AF.Copy, [], ["ap" + u], ["pw" + u])
-        act(T["yy" + u][:, :], T["aa" + u][:, C:2 * C], AF.Abs, ["ap" + u], ["yy" + u], bias=2.0 ** -125, scale=0.6 * 2.0 ** -23)
+        mm("pw" + u, k, T.st[:, s], T.ss[:, s], T["zq" + u][:, :], T["zs" + u][:, :], ["st" + u, "ss" + u, "zq" + u])
+
+    def plain(f):
+        act(T["ap%d" % f][:, :], T.pw[:, 512 * f:512 * f + C], AF.Copy, [], ["ap%d" % f], ["pw%d" % f])
+
+    def slot(f, c, a, b):
+        j, t = WHERE[c]
+        return T["ut%d" % f][:, 4 * (AT[j] + a) + t:4 * (AT[j] + b):4], ["u%d%d%d" % (f, j, t)]
 
     def prep(f):
         u = "%d" % f
         k = T.pw[:, 512 * f:512 * f + C]
         tt(T["mk" + u][:, :], k, T.mb[:, :], OP.min, ["mb"], ["mk" + u], ["pw" + u])
+        yield
         scan(T["sc" + u][:, :], T.rst[:, :], T["mk" + u][:, :], -BIG, OP.min, OP.max, ["rst", "mk" + u], ["sc" + u])
-        tt(T["aa" + u][:, 0:C], k, T["yy" + u][:, :], OP.subtract, ["yy" + u], ["am" + u], ["pw" + u])
-        if NS[f]:
-            act(T["nt" + u][:, :], T["sc" + u][:, 15:C:16], AF.Copy, ["sc" + u], ["nt" + u], scale=-1.0)
+        act(T["nt" + u][:, :], T["sc" + u][:, 15:C:16], AF.Copy, ["sc" + u], ["nt" + u], scale=-1.0)
+        yield
+        tt(T["ut" + u][:, 3:4 * C:4], k, T["sc" + u][:, :], OP.is_equal, ["sc" + u], ["u%d03" % f], ["pw" + u])
+        yield
 
-    def ties(f):
+    turn = [0, 0]
+
+    def alone(f, cs):
         u = "%d" % f
-        tt(T["ee" + u][:, :], T.pw[:, 512 * f:512 * f + C], T["sc" + u][:, :], OP.is_equal, ["sc" + u], ["ee" + u], ["pw" + u])
-        scan(T["xx" + u][:, :], T.hb[:, :], T["ee" + u][:, :], 0.0, OP.mult, OP.add, ["hb", "ee" + u], ["xx" + u])
 
-    def slot(f, c):
-        return T["cm%d" % f][:, C * c:C * c + C], ["cm%d%d" % (f, c)], ["rk%d%d" % (f, c)], T["aa%d" % f][:, 16 * c + 16:16 * c + 16 + C], T["rk%d" % f][:, c:c + 1]
+        def second(c, sg):
+            w = 16 * c
+            o, n = slot(f, c, 0, w)
+            act(o, T.sg[:, C * sg:C * sg + w], AF.Sign, ["sg%d" % sg], n + ["rk%s%d" % (u, c)], bias=0.5, accum_out=T["rk" + u][:, c:c + 1])
+            o, n = slot(f, c, w, w + 16)
+            act(o, T.sg[:, C * sg + w:C * sg + w + 16], AF.Sign, ["sg%d" % sg], ["own%s%d" % (u, c)], bias=0.5)
+        last = None
+        for c in cs:
+            sg, turn[0] = turn[0] % 4, turn[0] + 1
+            act(T.sg[:, C * sg:C * sg + 16 * c + 16], T["ap" + u][:, 0:16 * c + 16], AF.Sign, ["ap" + u, "nt" + u], ["sg%d" % sg], bias=T["nt" + u][:, c:c + 1])
+            if last:
+                second(*last)
+            last = (c, sg)
+        second(*last)
 
-    def alone(f, c):
-        m, cm, rk, w, o = slot(f, c)
-        act(m, w, AF.Sign, ["ap%d" % f, "am%d" % f, "nt%d" % f], cm, bias=T["nt%d" % f][:, c:c + 1])
-        act(m, m, AF.Sign, cm, cm + rk, bias=0.5, accum_out=o)
+    def compare(f, cs):
+        u = "%d" % f
+        for c in cs:
+            o, n = slot(f, c, 0, 16 * c + 16)
+            ts(o, T["ap" + u][:, 0:16 * c + 16], T["sc" + u][:, 16 * c + 15:16 * c + 16], None, OP.is_ge, None, ["ap" + u, "sc" + u], n)
+            yield
 
-    def compare(f, c):
-        m, cm, rk, w, o = slot(f, c)
-        ts(m, w, T["sc%d" % f][:, 16 * c + 15:16 * c + 16], None, OP.is_ge, None, ["ap%d" % f, "am%d" % f, "sc%d" % f], cm)
-        act(m, m, AF.Copy, cm, cm + rk, accum_out=o)
+    def addup(f):
+        for c in OWN:
+            if c:
+                o, n = slot(f, c, 0, 16 * c)
+                jk, turn[1] = turn[1] % 4, turn[1] + 1
+                act(T.jk[:, C * jk:C * jk + 16 * c], o, AF.Copy, n, ["jk%d" % jk, "rk%d%d" % (f, c)], scale=2.0, accum_out=T["rk%d" % f][:, c:c + 1])
+
+    def down(f, j):
+        u = "%d" % f
+        s = slice(AT[j], AT[j + 1])
+        quant(T["uq" + u][:, s], T["us" + u][:, s], T["ut" + u][:, 4 * AT[j]:4 * AT[j + 1]],
+              ["u%d%d%d" % (f, j, t) for t in range(4)] + ["own%s%d" % (u, c) for c in TILES[j]], ["uq%s%d" % (u, j)])
+        b, w = 2 + f, 0 if j == 0 else 256 if j == LAST else 128
+        mm("pw%d" % b, T.pw[:, 512 * b:512 * b + WIDE[j]], T.aq[:, w:w + 128], T.ax[:, w:w + 128], T["uq" + u][:, s], T["us" + u][:, s],
+           ["aq", "uq%s%d" % (u, j)], j == 0, j == LAST)
+        yield
 
     def survive(f, r):
         u = "%d" % f
         n = "%d%d" % (f, r)
-        tt(T["rr" + u][:, :], T["rk" + u][:, :], T["xx" + u][:, 15:C:16], OP.subtract, ["rk%d%d" % (f, c) for c in range(20)] + ["xx" + u], ["rr" + u])
-        tc(T["ro" + u][:, :], T["rr" + u][:, :], ["rr" + u], ["ro" + u])
+        b = 2 + f
+        tt(T["md" + u][:, :], T.pw[:, 512 * b:512 * b + C], T.m16[:, :], OP.mult, ["m16"], ["md" + u], ["pw%d" % b])
+        yield
+        scan(T["dd" + u][:, :], T.h16[:, :], T["md" + u][:, :], 0.0, OP.mult, OP.add, ["h16", "md" + u], ["dd" + u])
+        yield
+        tt(T["rr" + u][:, :], T["rk" + u][:, :], T.cc[:, :], OP.add, ["rk%d%d" % (f, c) for c in range(20)] + runs, ["rr" + u])
+        yield
+        tt(T["rs" + u][:, :], T["rr" + u][:, :], T["dd" + u][:, 15:C:16], OP.add, ["rr" + u, "dd" + u], ["rs" + u])
+        yield
+        ts(T["ro" + u][:, :], T["rs" + u][:, :], 0.5, None, OP.mult, None, ["rs" + u], ["ro" + u])
+        yield
         tc(T["inv" + u][:, :].indirect(T["ro" + u][:, 0:20]), T.i4[:, :], ["ro" + u, "i4"], ["inv" + u])
+        yield
         tt(T["gm" + u][:, :], T["inv" + u][:, 0:A], T.m4[:, :], OP.mult, ["inv" + u, "m4"], ["gm" + u])
+        yield
         scan(T["gn" + u][:, :], T.h4[:, :], T["gm" + u][:, :], 0.0, OP.mult, OP.add, ["gm" + u, "h4"], ["gn" + u])
+        yield
         ts(T["of4" + u][:, :], T["gn" + u][:, 3:A:4], T.qf[:, 2:3], None, OP.add, None, ["gn" + u, "qf"], ["of4" + u])
+        yield
         tc(T["pl" + u][:, 0:256], T["zt" + u][:, :].indirect(T["of4" + u][:, 0:16]), ["of4" + u] + ["zt" + u + "%d" % t for t in range(4)], ["pl" + u])
-        quant(T["pc" + n][:, :], T["pp" + n][:, :], T["pl" + u][:, :], ["pl" + u, "pz" + u], ["pc" + n])
+        yield
+        v = slice(128 * r, 128 * r + 128)
+        quant(T["pc" + u][:, v], T["pp" + u][:, v], T["pl" + u][:, :], ["pl" + u, "pz" + u], ["pc" + n])
         d = T.cores[(rank + 1 - 2 * f) % N]
         rid, pid = topo.addr(d, core)
         m, ne = topo.mask(core, d), len(topo.engines(core, d))
-        s, k = slice(64 * f, 64 * f + 64), "ar%d" % r
+        s, v, k = slice(64 * r + 64, 64 * r + 128), slice(128 * r, 128 * r + 64), "ar" + n
         need("G", ["pc" + n], [])
-        g.remote_dma(T["lc%d" % r][:, s].bitcast(dt.uint8), T["pc" + n][:, 0:64].bitcast(dt.uint8), T.sem[k], T.sem.ls, pid, rid, m)
-        g.remote_dma(T["lp%d" % r][:, s], T["pp" + n][:, 0:64], T.sem[k], T.sem.ls, pid, rid, m)
-        cnt["ls"] = cnt.get("ls", 0) + 2 * ne
-        cnt[k] = cnt.get(k, 0) + 2 * ne
+        g.remote_dma(T["lc" + u][:, s].bitcast(dt.uint8), T["pc" + u][:, v].bitcast(dt.uint8), T.sem[k], T.sem.ls, pid, rid, m)
+        g.remote_dma(T["lp" + u][:, s], T["pp" + u][:, v], T.sem[k], T.sem.ls, pid, rid, m)
+        cnt["ls"] += 2 * ne
+        cnt[k] = 2 * ne
+        yield
 
-    def etable(f):
+    def places(f):
         u = "%d" % f
         tt(T["em" + u][:, :], T["inv" + u][:, 0:A], T.m16[:, 0:A], OP.mult, ["inv" + u, "m16"], ["em" + u])
-        scan(T["en" + u][:, :], T.h16[:, :], T["em" + u][:, :], 0.0, OP.mult, OP.add, ["em" + u, "h16"], ["en" + u])
+        yield
+        scan(T["en" + u][:, :], T.h16[:, 0:A], T["em" + u][:, :], 0.0, OP.mult, OP.add, ["em" + u, "h16"], ["en" + u])
+        yield
         ts(T["eo" + u][:, :], T["en" + u][:, 15:A:16], 0.25, None, OP.mult, None, ["en" + u], ["eo" + u])
         s = slice(32 * f, 32 * f + 32)
         act(T.olo[:, s], T["oz" + u][:, :].indirect(T["eo" + u][:, 0:2]), AF.Copy, ["oz" + u, "eo" + u], ["olo" + u])
         act(T.ohi[:, s], T["oz" + u][:, :].indirect(T["eo" + u][:, 2:4]), AF.Copy, ["oz" + u, "eo" + u], ["ohi" + u], scale=64.0)
+        yield
+
+    def origins(f):
+        act(T["oz%d" % f][:, :], T.olf[:, :].indirect(T.op[:, 20 * f:20 * f + 20]), AF.Copy, ["olf", "op%d" % f], ["oz%d" % f])
 
     def origins_out(r):
         n = "%d" % r
         tt(T.osm[:, :], T.olo[:, :], T.ohi[:, :], OP.add, ["olo0", "olo1", "ohi0", "ohi1"], ["osm"])
-        tc(T["ou" + n][:, :], T.osm[:, :], ["osm"], ["ou" + n])
+        yield
+        tc(T.ou[:, 64 * r:64 * r + 64], T.osm[:, :], ["osm"], ["ou" + n])
         need("G", ["ou" + n], [])
         tr = []
         for f in range(2):
             d = T.cores[(rank + 1 - 2 * f) % N]
             rid, pid = topo.addr(d, core)
             en = topo.engines(core, d)
-            h, s = len(en) // 2, slice(32 * f, 32 * f + 32)
+            h, s = len(en) // 2, slice(64 * r + 32 * f, 64 * r + 32 * f + 32)
             tr.append(RemoteDMATransfer(dst_ids=[DstId(rid=rid, pnc=pid)], dma_engine_mask=sum(1 << e for e in en[h * f:h * f + h]),
-                                        remote_sem=T.sem["ao" + n], src=T["ou" + n][:, s], dst=T["on" + n][:, s]))
+                                        remote_sem=T.sem["ao" + n], src=T.ou[:, s], dst=T.on[:, s]))
             cnt["ls"] += h
             cnt["ao" + n] = cnt.get("ao" + n, 0) + h
         g.remote_dma_fused(tr, local_sem=T.sem.ls)
+        yield
 
     def origins_in(r, last):
         n = "%d" % r
         lastw["on" + n] = ("ao" + n, cnt["ao" + n])
-        tc(T.oi[:, :], T["on" + n][:, :], ["on" + n], ["oi"])
+        tc(T.oi[:, :], T.on[:, 64 * r:64 * r + 64], ["on" + n], ["oi"])
+        yield
         ts(T.oj[:, 0:64], T.oi[:, :], 63, None, OP.bitwise_and, None, ["oi"], ["oj0"])
         ts(T.oj[:, 64:128], T.oi[:, :], 6, None, OP.logical_shift_right, None, ["oi"], ["oj1"])
+        yield
         if not last:
             tc(T.olf[:, :], T.oj[:, :], ["oj0", "oj1"], ["olf"])
             return
@@ -279,85 +395,102 @@ def rank_program(g, core, T, topo):
                 ts(T.of[:, o:o + 32], T.oj[:, i:i + 32], base, None, OP.add, None, ["oj%d" % h], ["of%d%d" % (f, h)])
         dma("Y", T.ot[:, :], T.of[0:128:16, :], ["of00", "of01", "of10", "of11"], [], "do")
 
-    def renew(r):
-        last = r == R - 1
-        n = "%d" % r
+    def renew(h, r):
+        last, u = r == R - 1, "%d" % h
+        n = "%d%d" % (h, r)
         lastw["lc" + n] = ("ar" + n, cnt["ar" + n])
         W = [slice(128 * b, 128 * b + 128) for b in range(4)]
         P = [slice(512 * b, 512 * b + 128) for b in range(4)]
+        D = [slice(512 * b + 64, 512 * b + 128) for b in range(4)]
+        K = [slice(512 * b, 512 * b + 64) for b in range(4)]
+        B = [slice(64 * b + 256 * h, 64 * b + 256 * h + 64) for b in range(4)]
+        x, ft = slice(64 * r, 64 * r + 128), T["ft" + u]
         two = 2.0 if last else 1.0
         for b in range(4):
-            mm("pd%d" % b, T.pd[:, P[b]], T.eq[:, W[b]], T.es[:, W[b]], T["lc" + n][:, :], T["lp" + n][:, :], ["lc" + n, "eq"])
+            mm("pd%d" % b, T.pd[:, P[b]], T.eq[:, W[b]], T.es[:, W[b]], T["lc" + u][:, x], T["lp" + u][:, x], ["lc" + n, "eq", "pad" + u, "pae" + u])
         for b in range(4):
-            o, i = T.ft[:, b:512:4], T.pd[:, P[b]]
+            o, i = ft[:, b:256:4], T.pd[:, D[b]]
             if b % 2:
-                act(o, i, AF.Copy, [], ["ft%d" % b], ["pd%d" % b], scale=two)
+                act(o, i, AF.Copy, [], ["ft%s%d" % (u, b)], ["pd%d" % b], scale=two)
             else:
-                ts(o, i, two, None, OP.mult, None, [], ["ft%d" % b], ["pd%d" % b])
-        quant(T.fq[:, :], T.fs[:, :], T.ft[:, :], ["ft%d" % b for b in range(4)], ["fq"])
+                ts(o, i, two, None, OP.mult, None, [], ["ft%s%d" % (u, b)], ["pd%d" % b])
+                yield
+        quant(T["fq" + u][:, :], T["fs" + u][:, :], ft[:, :], ["ft%s%d" % (u, b) for b in range(4)] + ["fz" + u], ["fq" + u])
+        yield
         for b in range(4):
-            mm("pw%d" % b, T.pw[:, P[b]], T.wq[:, W[b]], T.wp[:, W[b]], T.fq[:, :], T.fs[:, :], ["wq", "wp", "fq"])
+            mm("pw%d" % b, T.pw[:, P[b]], T.wq[:, W[b]], T.wp[:, W[b]], T["fq" + u][:, :], T["fs" + u][:, :], ["wq", "wp", "fq" + u])
         for b in range(4):
-            act(T.rb[:, W[b]], T.pw[:, P[b]], AF.Relu, [], ["rb%d" % b], ["pw%d" % b], scale=0.03125)
+            act(T.rb[:, B[b]], T.pw[:, K[b]], AF.Relu, [], ["rb%s%d" % (u, b)], ["pw%d" % b], scale=0.03125)
         for b in range(4):
-            o = T.bt[:, b:512:4]
+            o, i = T.bt[:, 256 * h + b:256 * h + 256:4], T.rb[:, B[b]]
             if last:
-                tt(o, T.rb[:, W[b]], T.ft[:, b:512:4], OP.add, ["rb%d" % b, "ft%d" % b], ["bt%d" % b])
+                tt(o, i, ft[:, b:256:4], OP.add, ["rb%s%d" % (u, b), "ft%s%d" % (u, b)], ["b%s%d" % (u, b)])
             else:
-                tt(o, T.rb[:, W[b]], T.pd[:, P[b]], OP.add, ["rb%d" % b], ["bt%d" % b], ["pd%d" % b])
+                tt(o, i, T.pd[:, D[b]], OP.add, ["rb%s%d" % (u, b)], ["b%s%d" % (u, b)], ["pd%d" % b])
+            yield
 
     for r in range(R):
         if r == 0:
             constants()
             for t in range(4):
                 xgather("S" if t < 2 else "V", 0, t)
-        stationary()
-        for t in range(4):
-            cand(0, t)
-        score(0)
+        quant(T.sq[:, :], T.sp[:, :], T.bt[:, :], HALF[0] + HALF[1], ["sq"])
+        picks(0)
         if r == 0:
+            constants2()
             for t in range(4):
-                xgather("S" if t < 2 else "V", 1, t)
-        cand(1, 0)
-        cand(1, 1)
-        prep(0)
-        cand(1, 2)
-        cand(1, 3)
-        for c in range(NS[0]):
-            alone(0, c)
+                xgather("S", 1, t)
+            run(cand(0, (2, 3, 0, 1)))
+            run(zquant(0), constants3())
+        score(0)
+        plain(0)
+        picks(1)
+        run(cand(1, (0, 1)))
+        run(prep(0), cand(1, (2, 3)))
+        alone(0, TILES[0])
+        run(zquant(1))
         score(1)
-        ties(0)
+        z, p = compare(0, OWN), prep(1)
+        next(z)
+        next(p)
+        plain(1)
+        alone(0, TILES[LAST])
+        next(z)
+        next(p)
+        run(z)
+        run(p)
+        addup(0)
+        alone(1, TILES[0])
+        downs = [down(0, j) for j in [0] + REST]
         if r:
-            origins_in(r - 1, False)
-        for f in range(2):
-            act(T["oz%d" % f][:, :], T.olf[:, :].indirect(T.op[:, 20 * f:20 * f + 20]), AF.Copy, ["olf", "op%d" % f], ["oz%d" % f])
-        if NS[0]:
-            names = ["rk0%d" % c for c in range(NS[0])]
-            act(T.rk0[:, 0:NS[0]], T.rk0[:, 0:NS[0]], AF.Copy, names, names, bias=C / 2.0, scale=0.5)
-        for c in range(NS[0], 20):
-            compare(0, c)
-        prep(1)
-        ties(1)
-        for c in range(20):
-            if c == ZAT:
-                survive(0, r)
-            compare(1, c)
+            downs.insert(0, origins_in(r - 1, False))
+        run(*downs)
+        run(down(0, LAST))
+        alone(1, TILES[LAST])
+        run(survive(0, r), compare(1, OWN))
+        addup(1)
+        for j in [0] + REST + [LAST]:
+            run(down(1, j))
+        origins(0)
+        origins(1)
+        run(survive(1, r), places(0))
         if r == 0:
             quant(T.eq[:, :], T.es[:, :], T.et[:, :], ["et%d" % b for b in range(4)], ["eq"])
+        run(renew(0, r), chain(places(1), origins_out(r)))
+        if r == 0:
             quant(T.vq[:, :], T.vs[:, :], T.vt[:, :], ["vt"], ["vq"])
-        survive(1, r)
-        etable(0)
-        etable(1)
-        origins_out(r)
-        renew(r)
+        if r < R - 1:
+            run(cand(0, (0, 1, 2, 3)))
+            run(zquant(0))
+        run(renew(1, r))
 
-    quant(T.sq[:, :], T.sp[:, :], T.bt[:, :], BT, ["sq"])
+    quant(T.sq[:, :], T.sp[:, :], T.bt[:, :], HALF[0] + HALF[1], ["sq"])
     dma("Y", T.oc[:, :], T.sq[:, :].bitcast(dt.uint8), ["sq"], [], "do")
     mm("pw0", T.pw[:, 0:128], T.vq[:, :], T.vs[:, :], T.sq[:, :], T.sp[:, :], ["vq", "sq"])
     act(T.yo[:, :], T.pw[:, 0:128], AF.Copy, [], ["yo"], ["pw0"])
     dma("S", T.y[:, :], T.yo[:, :], ["yo"], [], "dy")
     for k in range(4):
         dma("Y", T.osc[4 * k:4 * k + 4, :], T.sp[32 * k:32 * k + 4, :], ["sq"], [], "do")
-    origins_in(R - 1, True)
+    run(origins_in(R - 1, True))
     for k in sorted(cnt):
         wait("G", k, cnt[k])

@@ -3,14 +3,14 @@ from concourse.mybir import dt, AluOpType, ActivationFunctionType
 
 N, C, A, R = 8, 320, 64, 3
 BIG = 2.0 ** 90
-TILES = [[19, 18, 17], [16, 15, 14, 13], [12, 11, 10, 9], [8, 7, 6, 5], [4, 3, 2, 1], [0]]
-WIDE = [C, 272, 208, 144, 128, 128]
-AT = [sum(WIDE[:j]) for j in range(7)]
-LAST = 2
-ALONE = TILES[0] + TILES[LAST]
-REST = [j for j in range(1, 6) if j != LAST]
-OWN = [c for j in REST for c in TILES[j]]
-WHERE = {c: (j, t) for j in range(6) for t, c in enumerate(TILES[j])}
+TILES = [[19, 18, 17], [16, 15, 14, 13], [12, 11, 10, 9], [8, 7, 6, 5], [4, 3, 2, 1]]
+WIDE = [C, 256, 192, 128, 128]
+NT = len(TILES)
+AT = [sum(WIDE[:j]) for j in range(NT + 1)]
+WHERE = {c: (j, t) for j in range(NT) for t, c in enumerate(TILES[j])}
+STEP, NEAR, SHIFT = 32767, 29000, 1536
+ALONE = [[0, 2], [0, 2]]
+CYC, WAKE, LEAD = 0.00083, 0.16, 5.5
 
 SCRATCH = {}
 
@@ -23,19 +23,20 @@ def sbuf(kind, **names):
 BF, F4, I4, U2, Q8, U1 = "bfloat16", "float32", "int32", "uint16", "float8_e4m3fn_x4", "uint8"
 sbuf(I4, li=80, lj=80, lk=80, pki=16, qi=4, qj=4, oi=64, oj=128)
 sbuf(U2, op=40, pk=16, off=320, ou=64 * R, on=64 * R)
-sbuf(BF, xt=4 * C, lr=512, bt=512, vt=512, et=2048, aw=1536, i8=512, zz=512, jk=4 * C, sg=4 * C)
-sbuf(Q8, vq=128, eq=512, aq=384, zc=128, wq=512, sq=128, st=256)
-sbuf(U1, vs=128, es=512, ax=384, zp=128, wp=512, sp=128, ss=256)
-sbuf(F4, rb=512, yo=128, qf=4, r16=C, r4=A, i4=C, m16=C, mb=C, rst=C, h16=C, m4=A, h4=A, olf=128, olo=64, ohi=64, osm=64, of=128, cc=20)
+sbuf(BF, xt=4 * C, lr=512, bt=512, vt=512, et=2048, aw=1536, i8=512, zz=512, jk=8 * C, sg=8 * C)
+sbuf(Q8, vq=128, eq=512, aq=384, zc=128, wq=512, sq=128, sl=128, st=256)
+sbuf(U1, vs=128, es=512, ax=384, zp=128, wp=512, sp=128, sm=128, ss=256)
+sbuf(F4, rb=512, yo=128, qf=4, qc=8, r16=C, r4=A, i4=C, m16=C, mb=C, rst=C, h16=C, d16=C, d4=A, olf=128, olo=64, ohi=64, osm=64, of=128)
 SCRATCH["pd"] = ("psum", [128, 2048], F4)
 SCRATCH["pw"] = ("psum", [128, 2048], F4)
 for _f in "01":
-    sbuf(BF, **{"xg" + _f: 4 * C, "zt" + _f: 4 * C, "pl" + _f: 512, "ft" + _f: 512, "ut" + _f: 4 * AT[6]})
-    sbuf(F4, **{"ap" + _f: C, "mk" + _f: C, "sc" + _f: C, "nt" + _f: 20, "rk" + _f: 20, "rr" + _f: 20, "rs" + _f: 20, "md" + _f: C, "dd" + _f: C,
-                "inv" + _f: C, "em" + _f: A, "en" + _f: A, "gm" + _f: A, "gn" + _f: A, "oz" + _f: C})
+    sbuf(BF, **{"xg" + _f: 4 * C, "zt" + _f: 4 * C, "pl" + _f: 512, "ft" + _f: 512, "ut" + _f: 4 * AT[NT]})
+    sbuf(F4, **{"mk" + _f: C, "sc" + _f: C, "nt" + _f: 20, "rk" + _f: 20, "rr" + _f: 20, "rs" + _f: 20, "dd" + _f: C,
+                "cc" + _f: 20, "ce" + _f: 20, "ow" + _f: C, "od" + _f: 20, "oe" + _f: 20,
+                "inv" + _f: C, "en" + _f: A, "gn" + _f: A, "oz" + _f: C})
     sbuf(U2, **{"ro" + _f: 20, "of4" + _f: 16, "eo" + _f: 4})
-    sbuf(Q8, **{"zq" + _f: C, "uq" + _f: AT[6], "fq" + _f: 128, "pc" + _f: 128 * R, "lc" + _f: 256})
-    sbuf(U1, **{"zs" + _f: C, "us" + _f: AT[6], "fs" + _f: 128, "pp" + _f: 128 * R, "lp" + _f: 256})
+    sbuf(Q8, **{"zq" + _f: C, "uq" + _f: AT[NT], "fq" + _f: 128, "pc" + _f: 128 * R, "lc" + _f: 256})
+    sbuf(U1, **{"zs" + _f: C, "us" + _f: AT[NT], "fs" + _f: 128, "pp" + _f: 128 * R, "lp" + _f: 256})
 SEMAPHORES = ["sV", "sS", "sT", "sG", "ls", "dl", "d0", "dx", "dw", "dv", "dz", "dy", "do", "ao0", "ao1", "ao2"]
 SEMAPHORES += ["ar%d%d" % (_f, _r) for _f in range(2) for _r in range(R)]
 
@@ -46,91 +47,153 @@ def rank_program(g, core, T, topo):
         return
     OP, AF = AluOpType, ActivationFunctionType
     Q = {"V": g.vector, "S": g.scalar, "T": g.tensor, "G": g, "Y": g.sync}
-    cnt, seen, snap, lastw, readers, lastx = {"ls": 0}, {e: {} for e in Q}, {}, {}, {}, {}
+    calls, lastw, readers, banks, total = [], {}, {}, {}, {}
 
-    def wait(e, k, n):
-        if seen[e].get(k, 0) >= n:
-            return
-        Q[e].wait_ge(T.sem[k], n)
-        seen[e][k] = n
-        for a, b in snap.get((k, n), {}).items():
-            if seen[e].get(a, 0) < b:
-                seen[e][a] = b
-
-    def need(e, rd, wr, ps=()):
-        own, want = "s" + e, {}
-        toks = [lastw[r] for r in list(rd) + list(wr) if r in lastw]
+    def add(e, f, rd, wr, ps, took, key, n, first=()):
+        deps, after, i = set(first), set(), len(calls)
+        for r in list(rd) + list(wr):
+            if r in lastw:
+                deps.add(lastw[r])
         for w in wr:
-            toks += readers.get(w, [])
-        toks += [lastx[p] for p in ps if p in lastx and lastx[p][0] != own]
-        for k, n in toks:
-            n = cnt[k] if k[0] == "d" else n
-            want[k] = max(n, want.get(k, 0))
-        for k in sorted(want):
-            wait(e, k, want[k])
-
-    def note(tok, e, rd, wr, ps=()):
-        snap[tok] = dict(seen[e])
-        for r in rd:
-            readers.setdefault(r, []).append(tok)
-        for w in wr:
-            lastw[w], readers[w] = tok, []
+            deps.update(readers.get(w, []))
         for p in ps:
-            lastx[p] = tok
+            for j in banks.get(p, []):
+                if calls[j]["e"] != e:
+                    deps.add(j)
+                elif e == "T":
+                    after.add(j)
+            banks.setdefault(p, []).append(i)
+        for r in rd:
+            readers.setdefault(r, []).append(i)
+        for w in wr:
+            lastw[w], readers[w] = i, []
+        calls.append({"e": e, "f": f, "deps": deps, "after": after - deps, "took": took, "key": key})
+        total[key] = total.get(key, 0) + n
+        return i
 
-    def op(e, f, rd, wr, ps=()):
-        need(e, rd, wr, ps)
-        k = "s" + e
-        cnt[k] = cnt.get(k, 0) + 1
-        f(Q[e]).then_inc(T.sem[k], 1)
-        note((k, cnt[k]), e, rd, wr, ps)
+    def op(e, f, rd, wr, ps, took):
+        add(e, f, rd, wr, ps, took, "s" + e, 1)
 
-    def tt(o, a, b, how, rd, wr, ps=()):
-        op("V", lambda q: q.tensor_tensor(o, a, b, how), rd, wr, ps)
+    def took(w, ind):
+        return 0.05 + w * CYC * 1.3 if ind else max(64, w) * CYC
 
-    def ts(o, a, s1, s2, o1, o2, rd, wr, ps=()):
+    def tt(o, a, b, how, w, rd, wr, ps=(), ind=False):
+        op("V", lambda q: q.tensor_tensor(o, a, b, how), rd, wr, ps, took(w if ps or ind else 2 * w, ind))
+
+    def ts(o, a, s1, s2, o1, o2, w, rd, wr, ps=(), ind=False):
         if o2 is None:
-            op("V", lambda q: q.tensor_scalar(o, a, s1, None, o1), rd, wr, ps)
+            op("V", lambda q: q.tensor_scalar(o, a, s1, None, o1), rd, wr, ps, took(w, ind))
         else:
-            op("V", lambda q: q.tensor_scalar(o, a, s1, s2, o1, o2), rd, wr, ps)
+            op("V", lambda q: q.tensor_scalar(o, a, s1, s2, o1, o2), rd, wr, ps, took(w, ind))
 
-    def tc(o, a, rd, wr, ps=()):
-        op("V", lambda q: q.tensor_copy(o, a), rd, wr, ps)
+    def tc(o, a, w, rd, wr, ps=(), ind=False):
+        op("V", lambda q: q.tensor_copy(o, a), rd, wr, ps, took(w, ind))
 
-    def fill(o, v, wr):
-        op("V", lambda q: q.memset(o, v), [], wr)
+    def fill(o, v, w, wr):
+        op("V", lambda q: q.memset(o, v), [], wr, (), took(w / 2, False))
 
-    def scan(o, a, b, first, o1, o2, rd, wr):
-        op("V", lambda q: q.tensor_tensor_scan(o, a, b, first, o1, o2), rd, wr)
+    def scan(o, a, b, first, o1, o2, w, rd, wr, ps=()):
+        op("V", lambda q: q.tensor_tensor_scan(o, a, b, first, o1, o2), rd, wr, ps, took(w, False))
 
-    def quant(c, s, t, rd, wr):
-        op("V", lambda q: q.quantize_mx(c, s, t), rd, wr)
+    def quant(c, s, t, w, rd, wr):
+        op("V", lambda q: q.quantize_mx(c, s, t), rd, wr, (), 0.012 + 0.00088 * w)
 
-    def act(o, i, func, rd, wr, ps=(), **kw):
-        op("S", lambda q: q.activation(o, i, func, **kw), rd, wr, ps)
+    def act(o, i, func, w, rd, wr, ps=(), ind=False, **kw):
+        op("S", lambda q: q.activation(o, i, func, **kw), rd, wr, ps, took(w, ind))
 
-    def mm(bank, o, w, ws, x, xs, rd, start=True, stop=True):
-        op("T", lambda q: q.matmul_mx(o, w, ws, x, xs, start, stop), rd, [], [bank])
+    def mm(bank, o, w, ws, x, xs, n, rd, start=True, stop=True):
+        op("T", lambda q: q.matmul_mx(o, w, ws, x, xs, start, stop), rd, [], [bank], (n + 16) * 0.001)
 
-    def dma(e, out, in_, rd, wr, k):
-        need(e, rd, wr)
-        cnt[k] = cnt.get(k, 0) + 16
-        Q[e].dma_start(out, in_).then_inc(T.sem[k], 16)
-        note((k, cnt[k]), e, rd, wr)
+    def dma(e, out, in_, rd, wr, k, took=2.2):
+        i = add(e, lambda q: q.dma_start(out, in_), rd, wr, (), 0.06, None, 0)
+        j = add("A", None, [], wr, (), took, k, 16, [i])
+        calls[i]["lands"] = j
+        for r in rd:
+            readers[r].append(j)
 
-    def iota(o, pattern, base, mult, wr, **kw):
-        op("G", lambda q: q.iota(o, pattern, base, mult, **kw), [], wr)
+    def iota(o, pattern, base, mult, w, wr, **kw):
+        op("G", lambda q: q.iota(o, pattern, base, mult, **kw), [], wr, (), 0.13 + 2 * w * CYC)
 
-    def run(*gens):
-        gens = list(gens)
-        while gens:
-            for x in list(gens):
-                if next(x, 1) is not None:
-                    gens.remove(x)
+    def send(f, rd, keys):
+        for k, n in keys:
+            total[k] = total.get(k, 0) + n
+        return add("G", f, rd, [], (), 0.9, None, 0)
 
-    def chain(*gens):
-        for x in gens:
-            yield from x
+    def came(first, wr, k, more=0.0):
+        calls[add("A", None, [], wr, (), 2.0, k, 0, first)]["more"] = more
+
+    def issue():
+        n, names = len(calls), list(Q) + ["A"]
+        users, left, far, early = [[] for _c in calls], [0] * n, [0.0] * n, [0.0] * n
+        for i, c in enumerate(calls):
+            for j in sorted(c["deps"] | c["after"]):
+                users[j].append(i)
+                left[i] += 1
+
+        def later(i, j):
+            return 0.0 if i in calls[j]["after"] else WAKE
+
+        for i in range(n - 1, -1, -1):
+            far[i] = calls[i]["took"] + calls[i].get("more", 0.0)
+            far[i] += max([far[j] + later(i, j) for j in users[i]], default=0.0)
+        ready, free, line = {e: [] for e in names}, {e: 0.0 for e in names}, []
+        for i in range(n):
+            if not left[i]:
+                ready[calls[i]["e"]].append(i)
+        while len(line) < n:
+            best = None
+            for e in names:
+                if ready[e]:
+                    i = min(ready[e], key=lambda j: early[j])
+                    t = early[i]
+                    if e != "A":
+                        t = max(t, free[e])
+                        i = max((j for j in ready[e] if early[j] <= t), key=lambda j: (far[j], -j))
+                    if best is None or t < best[0]:
+                        best = (t, i)
+            t, i = best
+            e = calls[i]["e"]
+            ready[e].remove(i)
+            line.append(i)
+            free[e] = t + calls[i]["took"]
+            for j in users[i]:
+                left[j] -= 1
+                early[j] = max(early[j], free[e] + later(i, j))
+                if not left[j]:
+                    ready[calls[j]["e"]].append(j)
+        cnt, seen, snap, tok = {}, {e: {} for e in Q}, {}, {}
+
+        def wait(e, k, m):
+            if seen[e].get(k, 0) < m:
+                Q[e].wait_ge(T.sem[k], m)
+                seen[e][k] = m
+                for a, b in snap.get((k, m), {}).items():
+                    if seen[e].get(a, 0) < b:
+                        seen[e][a] = b
+
+        for i in line:
+            c = calls[i]
+            e, want = c["e"], {}
+            if e == "A":
+                tok[i] = (c["key"], total[c["key"]])
+                continue
+            for j in c["deps"]:
+                if j in tok:
+                    k, m = tok[j]
+                    want[k] = max(m, want.get(k, 0))
+            for k in sorted(want):
+                wait(e, k, want[k])
+            x = c["f"](Q[e])
+            if c["key"]:
+                k = c["key"]
+                cnt[k] = cnt.get(k, 0) + 1
+                x.then_inc(T.sem[k], 1)
+                tok[i] = (k, cnt[k])
+                snap[tok[i]] = dict(seen[e])
+            elif "lands" in c:
+                x.then_inc(T.sem[calls[c["lands"]]["key"]], 16)
+        for k in sorted(k for k in total if k):
+            wait("G", k, total[k])
 
     HALF = [["b%d%d" % (h, b) for b in range(4)] for h in range(2)]
     LI = ["li0", "li1", "li2", "li3"]
@@ -139,232 +202,194 @@ def rank_program(g, core, T, topo):
         dma("S", T.li[:, 20 * i:20 * i + 20], T[nm][:, :], [], [LI[i]], "dl")
     dma("Y", T.lr[:, 0:256], T.l0[:, :], [], ["lr0"], "d0")
     dma("Y", T.lr[:, 256:512], T.r0[:, :], [], ["lr1"], "d0")
-    dma("Y", T.xt[:, :], T.x[:, :], [], ["xt"], "dx")
-    dma("Y", T.wq[:, :].bitcast(dt.uint8), T.wc[:, :], [], ["wq"], "dw")
-    dma("Y", T.wp[:, :], T.ws[:, :], [], ["wp"], "dw")
-    dma("Y", T.vt[:, :], T.v[:, :], [], ["vt"], "dv")
+    dma("Y", T.xt[:, :], T.x[:, :], [], ["xt"], "dx", 3.0)
+    dma("Y", T.wq[:, :].bitcast(dt.uint8), T.wc[:, :], [], ["wq"], "dw", 4.0)
+    dma("Y", T.wp[:, :], T.ws[:, :], [], ["wp"], "dw", 4.0)
+    dma("Y", T.vt[:, :], T.v[:, :], [], ["vt"], "dv", 5.0)
 
     big = {"allow_small_or_imprecise_dtypes": True}
-    iota(T.qi[:, 3:4], [[1, 1]], 0, 1, ["qi"])
-    iota(T.pki[:, 0:8], [[8, 8]], 64, 0, ["pki"])
-    iota(T.pki[:, 8:16], [[8, 8]], 0, 0, ["pki2"])
-    iota(T.r16[:, :], [[0, 20], [1, 16]], 0, 0, ["r16"], **big)
-    iota(T.r4[:, :], [[0, 16], [1, 4]], 0, 0, ["r4"], **big)
-    iota(T.i8[:, :], [[1, 8], [0, 64]], 0, 0, ["i8"], **big)
-    val = [2 * (16 * (20 - c) - 1 - 8 * sum(a >= c for a in ALONE)) + (16 * c if c in ALONE else 0) for c in range(20)]
-    runs, c = [], 0
-    while c < 20:
-        d, e = (val[c + 1] - val[c] if c < 19 else 0), c + 1
-        while e < 20 and val[e] - val[e - 1] == d:
-            e += 1
-        runs.append("cc%d" % c)
-        iota(T.cc[:, c:e], [[d, e - c]], val[c], 0, [runs[-1]], **big)
-        c = e
-    iota(T.i4[:, :], [[4, C]], 0, 0, ["i4"], **big)
-    iota(T.olf[:, :], [[32, 2], [0, 2], [1, 32]], 0, 0, ["olf"], **big)
-    fill(T.zz[:, :], 0.0, ["zz"])
+    iota(T.qi[:, 3:4], [[1, 1]], 0, 1, 1, ["qi"])
+    iota(T.pki[:, 0:8], [[8, 8]], 64, 0, 8, ["pki"])
+    iota(T.pki[:, 8:16], [[8, 8]], 0, 0, 8, ["pki2"])
+    iota(T.r16[:, :], [[0, 20], [STEP, 16]], 0, 0, C, ["r16"], **big)
+    iota(T.r4[:, :], [[0, 16], [STEP, 4]], 0, 0, A, ["r4"], **big)
+    iota(T.i8[:, :], [[1, 8], [0, 64]], 0, 0, 512, ["i8"], **big)
+    runs = [[], []]
+    for f in range(2):
+        al = [c for j in ALONE[f] for c in TILES[j]]
+        val = [2 * (16 * (19 - c) - 8 * sum(a > c for a in al) + 15) + (16 * c if c in al else 0) - 15 * SHIFT for c in range(20)]
+        c = 0
+        while c < 20:
+            d, e = (val[c + 1] - val[c] if c < 19 else 0), c + 1
+            while e < 20 and val[e] - val[e - 1] == d:
+                e += 1
+            runs[f].append("cc%d%d" % (f, c))
+            iota(T["cc%d" % f][:, c:e], [[d, e - c]], val[c], 0, e - c, [runs[f][-1]], **big)
+            c = e
+    iota(T.i4[:, :], [[4, C]], 0, 0, C, ["i4"], **big)
+    iota(T.olf[:, :], [[32, 2], [0, 2], [1, 32]], 0, 0, 128, ["olf"], **big)
+    fill(T.zz[:, :], 0.0, 512, ["zz"])
+
+    def column(b):
+        o = T.et[:, 512 * b:512 * b + 512]
+        op("G", lambda q: q.affine_select(o, T.zz[:, :], [[1, 512]], OP.not_equal, 0.5, -b, -4), ["zz"], ["et%d" % b], (), 1.02)
+
     for b in range(4):
-        e = T.et[:, 512 * b:512 * b + 512]
-        op("G", lambda q: q.affine_select(e, T.zz[:, :], [[1, 512]], OP.not_equal, 0.5, -b, -4), ["zz"], ["et%d" % b])
-    quant(T.zc[:, :], T.zp[:, :], T.zz[:, :], ["zz"], ["zc"])
+        column(b)
+    quant(T.zc[:, :], T.zp[:, :], T.zz[:, :], 128, ["zz"], ["zc"])
     for f in range(2):
         u = "%d" % f
         dma("Y", T["lc" + u][:, 0:64].bitcast(dt.uint8), T.zc[:, 0:64].bitcast(dt.uint8), ["zc"], ["pad" + u], "dz")
         dma("Y", T["lp" + u][:, 0:64], T.zp[:, 0:64], ["zc"], ["pae" + u], "dz")
-    tc(T.pk[:, :], T.pki[:, :], ["pki", "pki2"], ["pk"])
+    tc(T.pk[:, :], T.pki[:, :], 16, ["pki", "pki2"], ["pk"])
     for f in range(2):
         u = "%d" % f
-        for j in range(6):
-            z = T["ut" + u][:, 4 * (AT[j] + (16 * (TILES[j][-1] + 1) if j < 5 else 0)):4 * AT[j + 1]]
-            fill(z, 0.0, ["u%d%d%d" % (f, j, t) for t in range(4)])
-        fill(T["pl" + u][:, 256:512], 0.0, ["pz" + u])
-        fill(T["ft" + u][:, 256:512], 0.0, ["fz" + u])
-        fill(T["rk" + u][:, 0:1], 0.0, ["rk%s0" % u])
-
+        for j in range(NT):
+            a, b = 4 * (AT[j] + 16 * TILES[j][-1]), 4 * AT[j + 1]
+            fill(T["ut" + u][:, a:b], 0.0, b - a, ["u%d%d%d" % (f, j, t) for t in range(4)])
+        fill(T["pl" + u][:, 256:512], 0.0, 256, ["pz" + u])
+        fill(T["ft" + u][:, 256:512], 0.0, 256, ["fz" + u])
+        fill(T["rk" + u][:, 0:1], 0.0, 1, ["rk%s0" % u])
+    ts(T.qj[:, 0:1], T.qi[:, 3:4], 15, None, OP.bitwise_and, None, 1, ["qi"], ["qj0"])
+    ts(T.qj[:, 1:2], T.qi[:, 3:4], 2, 3, OP.logical_shift_right, OP.bitwise_and, 1, ["qi"], ["qj1"])
+    ts(T.qj[:, 2:3], T.qi[:, 3:4], 3, None, OP.bitwise_and, None, 1, ["qi"], ["qj2"])
+    ts(T.qj[:, 3:4], T.qi[:, 3:4], 4, None, OP.logical_shift_right, None, 1, ["qi"], ["qj3"])
+    tc(T.qf[:, :], T.qj[:, :], 4, ["qj0", "qj1", "qj2", "qj3"], ["qf"])
+    ts(T.qc[:, 0:1], T.qf[:, 0:1], float(STEP), None, OP.mult, None, 1, ["qf"], ["qc0"])
+    ts(T.qc[:, 1:2], T.qf[:, 0:1], float(STEP), float(NEAR), OP.mult, OP.add, 1, ["qf"], ["qc1"])
+    ts(T.qc[:, 2:3], T.qf[:, 1:2], float(STEP), float(NEAR), OP.mult, OP.add, 1, ["qf"], ["qc2"])
+    ts(T.m16[:, :], T.r16[:, :], T.qc[:, 0:1], 2 * BIG, OP.is_equal, OP.mult, C, ["r16", "qc0"], ["m16"])
+    ts(T.mb[:, :], T.m16[:, :], -BIG, None, OP.add, None, C, ["m16"], ["mb"])
+    ts(T.h16[:, :], T.r16[:, :], 0.0, None, OP.is_gt, None, C, ["r16"], ["h16"])
+    ts(T.rst[:, :], T.h16[:, :], 2 * BIG, -BIG, OP.mult, OP.add, C, ["h16"], ["rst"])
+    ts(T.d16[:, :], T.r16[:, :], T.qc[:, 1:2], float(SHIFT), OP.subtract, OP.min, C, ["r16", "qc1"], ["d16"])
+    ts(T.d4[:, :], T.r4[:, :], T.qc[:, 2:3], float(SHIFT), OP.subtract, OP.min, A, ["r4", "qc2"], ["d4"])
+    ts(T.qc[:, 3:4], T.qf[:, 0:1], float(SHIFT), -15.0 * SHIFT, OP.mult, OP.add, 1, ["qf"], ["qc3"])
+    ts(T.qc[:, 4:5], T.qf[:, 1:2], float(SHIFT), T.qf[:, 2:3], OP.mult, OP.add, 1, ["qf"], ["qc4"])
+    ts(T.qc[:, 5:6], T.qf[:, 0:1], float(SHIFT - 2), None, OP.mult, None, 1, ["qf"], ["qc5"])
+    for f in range(2):
+        ts(T["ce%d" % f][:, :], T["cc%d" % f][:, :], T.qc[:, 5:6], None, OP.add, None, 20, runs[f] + ["qc5"], ["ce%d" % f])
+    ts(T.aw[:, 512:1024], T.i8[:, :], T.qf[:, 3:4], -2.0, OP.is_equal, OP.mult, 512, ["i8", "qf"], ["aw1"])
+    act(T.aw[:, 0:512], T.aw[:, 512:1024], AF.Copy, 512, ["aw1"], ["aw0"], scale=0.5)
+    act(T.aw[:, 3:512:4], T.aw[:, 515:1024:4], AF.Copy, 128, ["aw1"], ["aw0"])
+    act(T.aw[:, 1024:1536], T.aw[:, 512:1024], AF.Copy, 512, ["aw1"], ["aw2"], scale=0.5)
+    quant(T.aq[:, :], T.ax[:, :], T.aw[:, :], 384, ["aw0", "aw1", "aw2"], ["aq"])
     for t in range(4):
-        ts(T.off[:, 80 * t:80 * t + 80], T.li[:, :], 4.0, float(t), OP.mult, OP.add, LI, ["ot%d" % t])
-    act(T.bt[:, 0:256], T.lr[:, 0:256], AF.Copy, ["lr0"], HALF[0], scale=0.5)
-    act(T.bt[:, 256:512], T.lr[:, 256:512], AF.Copy, ["lr1"], HALF[1], scale=0.5)
+        ts(T.off[:, 80 * t:80 * t + 80], T.li[:, :], 4.0, float(t), OP.mult, OP.add, 80, LI, ["ot%d" % t])
+    ts(T.lj[:, :], T.li[:, :], 32.0, 32.0, OP.is_ge, OP.mult, 80, LI, ["lj"])
+    tt(T.lk[:, :], T.lj[:, :], T.li[:, :], OP.add, 80, ["lj"] + LI, ["lk"])
+    tc(T.op[:, 0:20], T.lk[:, 0:20], 20, ["lk"], ["op0"])
+    ts(T.op[:, 20:40], T.lk[:, 40:60], 32.0, None, OP.add, None, 20, ["lk"], ["op1"])
+    act(T.bt[:, 0:256], T.lr[:, 0:256], AF.Copy, 256, ["lr0"], HALF[0], scale=0.5)
+    act(T.bt[:, 256:512], T.lr[:, 256:512], AF.Copy, 256, ["lr1"], HALF[1], scale=0.5)
 
     def xgather(e, f, t):
         o = T["xg%d" % f][:, C * t:C * t + C]
         w = T.xt[:, :].indirect(T.off[:, 80 * t + 40 * f + 20:80 * t + 40 * f + 40])
         if e == "S":
-            act(o, w, AF.Copy, ["xt", "ot%d" % t], ["xg%d%d" % (f, t)], scale=0.5)
+            act(o, w, AF.Copy, C, ["xt", "ot%d" % t], ["xg%d%d" % (f, t)], (), True, scale=0.5)
         else:
-            ts(o, w, 0.5, None, OP.mult, None, ["xt", "ot%d" % t], ["xg%d%d" % (f, t)])
+            ts(o, w, 0.5, None, OP.mult, None, C, ["xt", "ot%d" % t], ["xg%d%d" % (f, t)], (), True)
 
-    def constants():
-        ts(T.qj[:, 0:1], T.qi[:, 3:4], 15, None, OP.bitwise_and, None, ["qi"], ["qj0"])
-        ts(T.qj[:, 1:2], T.qi[:, 3:4], 2, 3, OP.logical_shift_right, OP.bitwise_and, ["qi"], ["qj1"])
-        ts(T.qj[:, 2:3], T.qi[:, 3:4], 3, None, OP.bitwise_and, None, ["qi"], ["qj2"])
-        ts(T.qj[:, 3:4], T.qi[:, 3:4], 4, None, OP.logical_shift_right, None, ["qi"], ["qj3"])
-        tc(T.qf[:, :], T.qj[:, :], ["qj0", "qj1", "qj2", "qj3"], ["qf"])
-        ts(T.m16[:, :], T.r16[:, :], T.qf[:, 0:1], None, OP.is_equal, None, ["r16", "qf"], ["m16"])
-        ts(T.h16[:, :], T.r16[:, :], 0.0, None, OP.is_gt, None, ["r16"], ["h16"])
-        ts(T.mb[:, :], T.m16[:, :], 2 * BIG, -BIG, OP.mult, OP.add, ["m16"], ["mb"])
-        ts(T.rst[:, :], T.h16[:, :], 2 * BIG, -BIG, OP.mult, OP.add, ["h16"], ["rst"])
-        ts(T.h4[:, :], T.r4[:, :], 0.0, None, OP.is_gt, None, ["r4"], ["h4"])
-        ts(T.m4[:, :], T.r4[:, :], T.qf[:, 1:2], None, OP.is_equal, None, ["r4", "qf"], ["m4"])
-        ts(T.aw[:, 512:1024], T.i8[:, :], T.qf[:, 3:4], -2.0, OP.is_equal, OP.mult, ["i8", "qf"], ["aw1"])
+    def side(q, x):
+        quant(T[q][:, :], T[x][:, :], T.bt[:, :], 128, HALF[0] + HALF[1], [q])
 
-    def constants2():
-        act(T.aw[:, 0:512], T.aw[:, 512:1024], AF.Copy, ["aw1"], ["aw0"], scale=0.5)
-        act(T.aw[:, 3:512:4], T.aw[:, 515:1024:4], AF.Copy, ["aw1"], ["aw0"], scale=-1.0)
-        act(T.aw[:, 1024:1536], T.aw[:, 512:1024], AF.Copy, ["aw1"], ["aw2"], scale=0.5)
-
-    def constants3():
-        quant(T.aq[:, :], T.ax[:, :], T.aw[:, :], ["aw0", "aw1", "aw2"], ["aq"])
-        yield
-        ts(T.lj[:, :], T.li[:, :], 32.0, 32.0, OP.is_ge, OP.mult, LI, ["lj"])
-        yield
-        tt(T.lk[:, :], T.lj[:, :], T.li[:, :], OP.add, ["lj"] + LI, ["lk"])
-        yield
-        tc(T.op[:, 0:20], T.lk[:, 0:20], ["lk"], ["op0"])
-        ts(T.op[:, 20:40], T.lk[:, 40:60], 32.0, None, OP.add, None, ["lk"], ["op1"])
-
-    def picks(f):
+    def picks(f, q, x):
         s, k = slice(128 * f, 128 * f + 128), T.pk[:, 8 * f:8 * f + 8]
-        tc(T.st[:, s].bitcast(dt.uint32), T.sq[:, 0:128].bitcast(dt.uint32).indirect(k), ["sq", "pk"], ["st%d" % f])
-        act(T.ss[:, s], T.sp[:, 0:128].indirect(k), AF.Copy, ["sq", "pk"], ["ss%d" % f])
+        tc(T.st[:, s].bitcast(dt.uint32), T[q][:, 0:128].bitcast(dt.uint32).indirect(k), 128, [q, "pk"], ["st%d" % f], (), True)
+        act(T.ss[:, s], T[x][:, 0:128].indirect(k), AF.Copy, 128, [q, "pk"], ["ss%d" % f], (), True)
 
-    def cand(f, quarters):
-        for t in quarters:
-            w = T.bt[:, 256 * f:256 * f + 256].indirect(T.off[:, 80 * t + 40 * f:80 * t + 40 * f + 20])
-            tt(T["zt%d" % f][:, t:4 * C:4], w, T["xg%d" % f][:, C * t:C * t + C], OP.add, HALF[f] + ["ot%d" % t, "xg%d%d" % (f, t)], ["zt%d%d" % (f, t)])
-            yield
-
-    def zquant(f):
+    def cand(f):
         u = "%d" % f
-        quant(T["zq" + u][:, :], T["zs" + u][:, :], T["zt" + u][:, :], ["zt" + u + "%d" % t for t in range(4)], ["zq" + u])
-        yield
+        for t in range(4):
+            w = T.bt[:, 256 * f:256 * f + 256].indirect(T.off[:, 80 * t + 40 * f:80 * t + 40 * f + 20])
+            tt(T["zt" + u][:, t:4 * C:4], w, T["xg" + u][:, C * t:C * t + C], OP.add, C, HALF[f] + ["ot%d" % t, "xg%d%d" % (f, t)], ["zt%d%d" % (f, t)], (), True)
+        quant(T["zq" + u][:, :], T["zs" + u][:, :], T["zt" + u][:, :], C, ["zt" + u + "%d" % t for t in range(4)], ["zq" + u])
 
     def score(f):
         u = "%d" % f
-        s, k = slice(128 * f, 128 * f + 128), T.pw[:, 512 * f:512 * f + C]
-        mm("pw" + u, k, T.st[:, s], T.ss[:, s], T["zq" + u][:, :], T["zs" + u][:, :], ["st" + u, "ss" + u, "zq" + u])
+        s = slice(128 * f, 128 * f + 128)
+        for b in ("pw", "pd"):
+            mm(b + u, T[b][:, 512 * f:512 * f + C], T.st[:, s], T.ss[:, s], T["zq" + u][:, :], T["zs" + u][:, :], C, ["st" + u, "ss" + u, "zq" + u])
 
-    def plain(f):
-        act(T["ap%d" % f][:, :], T.pw[:, 512 * f:512 * f + C], AF.Copy, [], ["ap%d" % f], ["pw%d" % f])
-
-    def slot(f, c, a, b):
+    def slot(f, c):
         j, t = WHERE[c]
-        return T["ut%d" % f][:, 4 * (AT[j] + a) + t:4 * (AT[j] + b):4], ["u%d%d%d" % (f, j, t)]
+        return T["ut%d" % f][:, 4 * AT[j] + t:4 * (AT[j] + 16 * c):4], ["u%d%d%d" % (f, j, t)]
 
     def prep(f):
         u = "%d" % f
-        k = T.pw[:, 512 * f:512 * f + C]
-        tt(T["mk" + u][:, :], k, T.mb[:, :], OP.min, ["mb"], ["mk" + u], ["pw" + u])
-        yield
-        scan(T["sc" + u][:, :], T.rst[:, :], T["mk" + u][:, :], -BIG, OP.min, OP.max, ["rst", "mk" + u], ["sc" + u])
-        act(T["nt" + u][:, :], T["sc" + u][:, 15:C:16], AF.Copy, ["sc" + u], ["nt" + u], scale=-1.0)
-        yield
-        tt(T["ut" + u][:, 3:4 * C:4], k, T["sc" + u][:, :], OP.is_equal, ["sc" + u], ["u%d03" % f], ["pw" + u])
-        yield
+        k, o = T.pw[:, 512 * f:512 * f + C], T["ut" + u][:, 3:4 * C:4]
+        tt(T["mk" + u][:, :], k, T.mb[:, :], OP.min, C, ["mb"], ["mk" + u], ["pw" + u])
+        scan(T["sc" + u][:, :], T.rst[:, :], T["mk" + u][:, :], -BIG, OP.min, OP.max, C, ["rst", "mk" + u], ["sc" + u])
+        act(T["nt" + u][:, :], T["sc" + u][:, 15:C:16], AF.Copy, 20, ["sc" + u], ["nt" + u], scale=-1.0)
+        tt(o, k, T["sc" + u][:, :], OP.is_gt, C, ["sc" + u], ["u%d03" % f], ["pw" + u])
+        scan(T["ow" + u][:, :], T.h16[:, :], o, 0.0, OP.mult, OP.add, C, ["h16", "u%d03" % f], ["ow" + u])
+        act(T["od" + u][:, :], T["ow" + u][:, 15:C:16], AF.Copy, 20, ["ow" + u], ["od" + u], scale=2.0)
+        tt(T["oe" + u][:, :], T["od" + u][:, :], T["ce" + u][:, :], OP.add, 20, ["od" + u, "ce" + u], ["oe" + u])
 
     turn = [0, 0]
 
-    def alone(f, cs):
+    def pairs(f):
         u = "%d" % f
-
-        def second(c, sg):
-            w = 16 * c
-            o, n = slot(f, c, 0, w)
-            act(o, T.sg[:, C * sg:C * sg + w], AF.Sign, ["sg%d" % sg], n + ["rk%s%d" % (u, c)], bias=0.5, accum_out=T["rk" + u][:, c:c + 1])
-            o, n = slot(f, c, w, w + 16)
-            act(o, T.sg[:, C * sg + w:C * sg + w + 16], AF.Sign, ["sg%d" % sg], ["own%s%d" % (u, c)], bias=0.5)
-        last = None
-        for c in cs:
-            sg, turn[0] = turn[0] % 4, turn[0] + 1
-            act(T.sg[:, C * sg:C * sg + 16 * c + 16], T["ap" + u][:, 0:16 * c + 16], AF.Sign, ["ap" + u, "nt" + u], ["sg%d" % sg], bias=T["nt" + u][:, c:c + 1])
-            if last:
-                second(*last)
-            last = (c, sg)
-        second(*last)
-
-    def compare(f, cs):
-        u = "%d" % f
-        for c in cs:
-            o, n = slot(f, c, 0, 16 * c + 16)
-            ts(o, T["ap" + u][:, 0:16 * c + 16], T["sc" + u][:, 16 * c + 15:16 * c + 16], None, OP.is_ge, None, ["ap" + u, "sc" + u], n)
-            yield
-
-    def addup(f):
-        for c in OWN:
-            if c:
-                o, n = slot(f, c, 0, 16 * c)
-                jk, turn[1] = turn[1] % 4, turn[1] + 1
-                act(T.jk[:, C * jk:C * jk + 16 * c], o, AF.Copy, n, ["jk%d" % jk, "rk%d%d" % (f, c)], scale=2.0, accum_out=T["rk%d" % f][:, c:c + 1])
-
-    def down(f, j):
-        u = "%d" % f
-        s = slice(AT[j], AT[j + 1])
-        quant(T["uq" + u][:, s], T["us" + u][:, s], T["ut" + u][:, 4 * AT[j]:4 * AT[j + 1]],
-              ["u%d%d%d" % (f, j, t) for t in range(4)] + ["own%s%d" % (u, c) for c in TILES[j]], ["uq%s%d" % (u, j)])
-        b, w = 2 + f, 0 if j == 0 else 256 if j == LAST else 128
-        mm("pw%d" % b, T.pw[:, 512 * b:512 * b + WIDE[j]], T.aq[:, w:w + 128], T.ax[:, w:w + 128], T["uq" + u][:, s], T["us" + u][:, s],
-           ["aq", "uq%s%d" % (u, j)], j == 0, j == LAST)
-        yield
+        for j in range(NT):
+            for c in TILES[j]:
+                w = 16 * c
+                k = T["pd" if j in ALONE[f] else "pw"][:, 512 * f:512 * f + w]
+                o, n = slot(f, c)
+                if j in ALONE[f]:
+                    m, turn[0] = turn[0] % 8, turn[0] + 1
+                    x = T.sg[:, C * m:C * m + w]
+                    act(x, k, AF.Sign, w, ["nt" + u], ["sg%d" % m], ["pd" + u], bias=T["nt" + u][:, c:c + 1])
+                    act(o, x, AF.Sign, w, ["sg%d" % m], n + ["rk%s%d" % (u, c)], bias=0.5, accum_out=T["rk" + u][:, c:c + 1])
+                else:
+                    m, turn[1] = turn[1] % 8, turn[1] + 1
+                    ts(o, k, T["sc" + u][:, w + 15:w + 16], None, OP.is_ge, None, w, ["sc" + u], n, ["pw" + u])
+                    act(T.jk[:, C * m:C * m + w], o, AF.Copy, w, n, ["jk%d" % m, "rk%s%d" % (u, c)], scale=2.0, accum_out=T["rk" + u][:, c:c + 1])
+            s = slice(AT[j], AT[j + 1])
+            quant(T["uq" + u][:, s], T["us" + u][:, s], T["ut" + u][:, 4 * AT[j]:4 * AT[j + 1]], WIDE[j], ["u%d%d%d" % (f, j, t) for t in range(4)], ["uq%s%d" % (u, j)])
+            b, w = 2 + f, 128 if j not in ALONE[f] else 256 if j else 0
+            mm("pw%d" % b, T.pw[:, 512 * b:512 * b + WIDE[j]], T.aq[:, w:w + 128], T.ax[:, w:w + 128], T["uq" + u][:, s], T["us" + u][:, s],
+               WIDE[j], ["aq", "uq%s%d" % (u, j)], j == 0, j == NT - 1)
 
     def survive(f, r):
         u = "%d" % f
         n = "%d%d" % (f, r)
         b = 2 + f
-        tt(T["md" + u][:, :], T.pw[:, 512 * b:512 * b + C], T.m16[:, :], OP.mult, ["m16"], ["md" + u], ["pw%d" % b])
-        yield
-        scan(T["dd" + u][:, :], T.h16[:, :], T["md" + u][:, :], 0.0, OP.mult, OP.add, ["h16", "md" + u], ["dd" + u])
-        yield
-        tt(T["rr" + u][:, :], T["rk" + u][:, :], T.cc[:, :], OP.add, ["rk%d%d" % (f, c) for c in range(20)] + runs, ["rr" + u])
-        yield
-        tt(T["rs" + u][:, :], T["rr" + u][:, :], T["dd" + u][:, 15:C:16], OP.add, ["rr" + u, "dd" + u], ["rs" + u])
-        yield
-        ts(T["ro" + u][:, :], T["rs" + u][:, :], 0.5, None, OP.mult, None, ["rs" + u], ["ro" + u])
-        yield
-        tc(T["inv" + u][:, :].indirect(T["ro" + u][:, 0:20]), T.i4[:, :], ["ro" + u, "i4"], ["inv" + u])
-        yield
-        tt(T["gm" + u][:, :], T["inv" + u][:, 0:A], T.m4[:, :], OP.mult, ["inv" + u, "m4"], ["gm" + u])
-        yield
-        scan(T["gn" + u][:, :], T.h4[:, :], T["gm" + u][:, :], 0.0, OP.mult, OP.add, ["gm" + u, "h4"], ["gn" + u])
-        yield
-        ts(T["of4" + u][:, :], T["gn" + u][:, 3:A:4], T.qf[:, 2:3], None, OP.add, None, ["gn" + u, "qf"], ["of4" + u])
-        yield
-        tc(T["pl" + u][:, 0:256], T["zt" + u][:, :].indirect(T["of4" + u][:, 0:16]), ["of4" + u] + ["zt" + u + "%d" % t for t in range(4)], ["pl" + u])
-        yield
+        tt(T["rr" + u][:, :], T["rk" + u][:, :], T["oe" + u][:, :], OP.add, 20, ["rk%d%d" % (f, c) for c in range(20)] + ["oe" + u], ["rr" + u])
+        scan(T["dd" + u][:, :], T.d16[:, :], T.pw[:, 512 * b:512 * b + C], 0.0, OP.add, OP.max, C, ["d16"], ["dd" + u], ["pw%d" % b])
+        tt(T["rs" + u][:, :], T["rr" + u][:, :], T["dd" + u][:, 15:C:16], OP.add, 20, ["rr" + u, "dd" + u], ["rs" + u])
+        ts(T["ro" + u][:, :], T["rs" + u][:, :], 0.5, None, OP.mult, None, 20, ["rs" + u], ["ro" + u])
+        tc(T["inv" + u][:, :].indirect(T["ro" + u][:, 0:20]), T.i4[:, :], 2.4 * C, ["ro" + u, "i4"], ["inv" + u], (), True)
+        scan(T["gn" + u][:, :], T.d4[:, :], T["inv" + u][:, 0:A], 0.0, OP.add, OP.max, A, ["inv" + u, "d4"], ["gn" + u])
+        ts(T["of4" + u][:, :], T["gn" + u][:, 3:A:4], T.qc[:, 4:5], -3.0 * SHIFT, OP.add, OP.add, 16, ["gn" + u, "qc4"], ["of4" + u])
+        tc(T["pl" + u][:, 0:256], T["zt" + u][:, :].indirect(T["of4" + u][:, 0:16]), 256, ["of4" + u] + ["zt" + u + "%d" % t for t in range(4)], ["pl" + u], (), True)
         v = slice(128 * r, 128 * r + 128)
-        quant(T["pc" + u][:, v], T["pp" + u][:, v], T["pl" + u][:, :], ["pl" + u, "pz" + u], ["pc" + n])
+        quant(T["pc" + u][:, v], T["pp" + u][:, v], T["pl" + u][:, :], 128, ["pl" + u, "pz" + u], ["pc" + n])
         d = T.cores[(rank + 1 - 2 * f) % N]
         rid, pid = topo.addr(d, core)
         m, ne = topo.mask(core, d), len(topo.engines(core, d))
         s, v, k = slice(64 * r + 64, 64 * r + 128), slice(128 * r, 128 * r + 64), "ar" + n
-        need("G", ["pc" + n], [])
-        g.remote_dma(T["lc" + u][:, s].bitcast(dt.uint8), T["pc" + u][:, v].bitcast(dt.uint8), T.sem[k], T.sem.ls, pid, rid, m)
-        g.remote_dma(T["lp" + u][:, s], T["pp" + u][:, v], T.sem[k], T.sem.ls, pid, rid, m)
-        cnt["ls"] += 2 * ne
-        cnt[k] = 2 * ne
-        yield
+        keys = [("ls", ne), (k, ne)]
+        i = send(lambda q: q.remote_dma(T["lc" + u][:, s].bitcast(dt.uint8), T["pc" + u][:, v].bitcast(dt.uint8), T.sem[k], T.sem.ls, pid, rid, m), ["pc" + n], keys)
+        j = send(lambda q: q.remote_dma(T["lp" + u][:, s], T["pp" + u][:, v], T.sem[k], T.sem.ls, pid, rid, m), ["pc" + n], keys)
+        came([i, j], ["lc" + n], k, LEAD * (1 - f))
 
     def places(f):
         u = "%d" % f
-        tt(T["em" + u][:, :], T["inv" + u][:, 0:A], T.m16[:, 0:A], OP.mult, ["inv" + u, "m16"], ["em" + u])
-        yield
-        scan(T["en" + u][:, :], T.h16[:, 0:A], T["em" + u][:, :], 0.0, OP.mult, OP.add, ["em" + u, "h16"], ["en" + u])
-        yield
-        ts(T["eo" + u][:, :], T["en" + u][:, 15:A:16], 0.25, None, OP.mult, None, ["en" + u], ["eo" + u])
+        scan(T["en" + u][:, :], T.d16[:, 0:A], T["inv" + u][:, 0:A], 0.0, OP.add, OP.max, A, ["inv" + u, "d16"], ["en" + u])
+        ts(T["eo" + u][:, :], T["en" + u][:, 15:A:16], T.qc[:, 3:4], 0.25, OP.add, OP.mult, 4, ["en" + u, "qc3"], ["eo" + u])
         s = slice(32 * f, 32 * f + 32)
-        act(T.olo[:, s], T["oz" + u][:, :].indirect(T["eo" + u][:, 0:2]), AF.Copy, ["oz" + u, "eo" + u], ["olo" + u])
-        act(T.ohi[:, s], T["oz" + u][:, :].indirect(T["eo" + u][:, 2:4]), AF.Copy, ["oz" + u, "eo" + u], ["ohi" + u], scale=64.0)
-        yield
+        act(T.olo[:, s], T["oz" + u][:, :].indirect(T["eo" + u][:, 0:2]), AF.Copy, 32, ["oz" + u, "eo" + u], ["olo" + u], (), True)
+        act(T.ohi[:, s], T["oz" + u][:, :].indirect(T["eo" + u][:, 2:4]), AF.Copy, 32, ["oz" + u, "eo" + u], ["ohi" + u], (), True, scale=64.0)
 
     def origins(f):
-        act(T["oz%d" % f][:, :], T.olf[:, :].indirect(T.op[:, 20 * f:20 * f + 20]), AF.Copy, ["olf", "op%d" % f], ["oz%d" % f])
+        act(T["oz%d" % f][:, :], T.olf[:, :].indirect(T.op[:, 20 * f:20 * f + 20]), AF.Copy, C, ["olf", "op%d" % f], ["oz%d" % f], (), True)
 
     def origins_out(r):
         n = "%d" % r
-        tt(T.osm[:, :], T.olo[:, :], T.ohi[:, :], OP.add, ["olo0", "olo1", "ohi0", "ohi1"], ["osm"])
-        yield
-        tc(T.ou[:, 64 * r:64 * r + 64], T.osm[:, :], ["osm"], ["ou" + n])
-        need("G", ["ou" + n], [])
-        tr = []
+        tt(T.osm[:, :], T.olo[:, :], T.ohi[:, :], OP.add, 64, ["olo0", "olo1", "ohi0", "ohi1"], ["osm"])
+        tc(T.ou[:, 64 * r:64 * r + 64], T.osm[:, :], 64, ["osm"], ["ou" + n])
+        tr, keys = [], []
         for f in range(2):
             d = T.cores[(rank + 1 - 2 * f) % N]
             rid, pid = topo.addr(d, core)
@@ -372,33 +397,28 @@ def rank_program(g, core, T, topo):
             h, s = len(en) // 2, slice(64 * r + 32 * f, 64 * r + 32 * f + 32)
             tr.append(RemoteDMATransfer(dst_ids=[DstId(rid=rid, pnc=pid)], dma_engine_mask=sum(1 << e for e in en[h * f:h * f + h]),
                                         remote_sem=T.sem["ao" + n], src=T.ou[:, s], dst=T.on[:, s]))
-            cnt["ls"] += h
-            cnt["ao" + n] = cnt.get("ao" + n, 0) + h
-        g.remote_dma_fused(tr, local_sem=T.sem.ls)
-        yield
+            keys += [("ls", h), ("ao" + n, h)]
+        i = send(lambda q: q.remote_dma_fused(tr, local_sem=T.sem.ls), ["ou" + n], keys)
+        came([i], ["on" + n], "ao" + n)
 
     def origins_in(r, last):
         n = "%d" % r
-        lastw["on" + n] = ("ao" + n, cnt["ao" + n])
-        tc(T.oi[:, :], T.on[:, 64 * r:64 * r + 64], ["on" + n], ["oi"])
-        yield
-        ts(T.oj[:, 0:64], T.oi[:, :], 63, None, OP.bitwise_and, None, ["oi"], ["oj0"])
-        ts(T.oj[:, 64:128], T.oi[:, :], 6, None, OP.logical_shift_right, None, ["oi"], ["oj1"])
-        yield
+        tc(T.oi[:, :], T.on[:, 64 * r:64 * r + 64], 64, ["on" + n], ["oi"])
+        ts(T.oj[:, 0:64], T.oi[:, :], 63, None, OP.bitwise_and, None, 64, ["oi"], ["oj0"])
+        ts(T.oj[:, 64:128], T.oi[:, :], 6, None, OP.logical_shift_right, None, 64, ["oi"], ["oj1"])
         if not last:
-            tc(T.olf[:, :], T.oj[:, :], ["oj0", "oj1"], ["olf"])
+            tc(T.olf[:, :], T.oj[:, :], 128, ["oj0", "oj1"], ["olf"])
             return
         for f in range(2):
             base = float(A * ((rank - R + 2 * R * f) % N))
             for h in range(2):
                 o, i = 64 * f + 32 * h, 64 * h + 32 * f
-                ts(T.of[:, o:o + 32], T.oj[:, i:i + 32], base, None, OP.add, None, ["oj%d" % h], ["of%d%d" % (f, h)])
+                ts(T.of[:, o:o + 32], T.oj[:, i:i + 32], base, None, OP.add, None, 32, ["oj%d" % h], ["of%d%d" % (f, h)])
         dma("Y", T.ot[:, :], T.of[0:128:16, :], ["of00", "of01", "of10", "of11"], [], "do")
 
     def renew(h, r):
         last, u = r == R - 1, "%d" % h
         n = "%d%d" % (h, r)
-        lastw["lc" + n] = ("ar" + n, cnt["ar" + n])
         W = [slice(128 * b, 128 * b + 128) for b in range(4)]
         P = [slice(512 * b, 512 * b + 128) for b in range(4)]
         D = [slice(512 * b + 64, 512 * b + 128) for b in range(4)]
@@ -407,90 +427,68 @@ def rank_program(g, core, T, topo):
         x, ft = slice(64 * r, 64 * r + 128), T["ft" + u]
         two = 2.0 if last else 1.0
         for b in range(4):
-            mm("pd%d" % b, T.pd[:, P[b]], T.eq[:, W[b]], T.es[:, W[b]], T["lc" + u][:, x], T["lp" + u][:, x], ["lc" + n, "eq", "pad" + u, "pae" + u])
+            mm("pd%d" % b, T.pd[:, P[b]], T.eq[:, W[b]], T.es[:, W[b]], T["lc" + u][:, x], T["lp" + u][:, x], 128, ["lc" + n, "eq", "pad" + u, "pae" + u])
         for b in range(4):
             o, i = ft[:, b:256:4], T.pd[:, D[b]]
             if b % 2:
-                act(o, i, AF.Copy, [], ["ft%s%d" % (u, b)], ["pd%d" % b], scale=two)
+                act(o, i, AF.Copy, 64, [], ["ft%s%d" % (u, b)], ["pd%d" % b], scale=two)
             else:
-                ts(o, i, two, None, OP.mult, None, [], ["ft%s%d" % (u, b)], ["pd%d" % b])
-                yield
-        quant(T["fq" + u][:, :], T["fs" + u][:, :], ft[:, :], ["ft%s%d" % (u, b) for b in range(4)] + ["fz" + u], ["fq" + u])
-        yield
+                ts(o, i, two, None, OP.mult, None, 64, [], ["ft%s%d" % (u, b)], ["pd%d" % b])
+        quant(T["fq" + u][:, :], T["fs" + u][:, :], ft[:, :], 128, ["ft%s%d" % (u, b) for b in range(4)] + ["fz" + u], ["fq" + u])
         for b in range(4):
-            mm("pw%d" % b, T.pw[:, P[b]], T.wq[:, W[b]], T.wp[:, W[b]], T["fq" + u][:, :], T["fs" + u][:, :], ["wq", "wp", "fq" + u])
+            mm("pw%d" % b, T.pw[:, P[b]], T.wq[:, W[b]], T.wp[:, W[b]], T["fq" + u][:, :], T["fs" + u][:, :], 128, ["wq", "wp", "fq" + u])
         for b in range(4):
-            act(T.rb[:, B[b]], T.pw[:, K[b]], AF.Relu, [], ["rb%s%d" % (u, b)], ["pw%d" % b], scale=0.03125)
+            act(T.rb[:, B[b]], T.pw[:, K[b]], AF.Relu, 64, [], ["rb%s%d" % (u, b)], ["pw%d" % b], scale=0.03125)
         for b in range(4):
             o, i = T.bt[:, 256 * h + b:256 * h + 256:4], T.rb[:, B[b]]
             if last:
-                tt(o, i, ft[:, b:256:4], OP.add, ["rb%s%d" % (u, b), "ft%s%d" % (u, b)], ["b%s%d" % (u, b)])
+                tt(o, i, ft[:, b:256:4], OP.add, 64, ["rb%s%d" % (u, b), "ft%s%d" % (u, b)], ["b%s%d" % (u, b)])
             else:
-                tt(o, i, T.pd[:, D[b]], OP.add, ["rb%s%d" % (u, b)], ["b%s%d" % (u, b)], ["pd%d" % b])
-            yield
+                tt(o, i, T.pd[:, D[b]], OP.add, 64, ["rb%s%d" % (u, b)], ["b%s%d" % (u, b)], ["pd%d" % b])
 
+    for t in range(4):
+        xgather("S" if t < 2 else "V", 0, t)
+    for t in range(4):
+        xgather("S", 1, t)
+    cand(0)
+    side("sq", "sp")
+    picks(1, "sq", "sp")
     for r in range(R):
-        if r == 0:
-            constants()
-            for t in range(4):
-                xgather("S" if t < 2 else "V", 0, t)
-        quant(T.sq[:, :], T.sp[:, :], T.bt[:, :], HALF[0] + HALF[1], ["sq"])
-        picks(0)
-        if r == 0:
-            constants2()
-            for t in range(4):
-                xgather("S", 1, t)
-            run(cand(0, (2, 3, 0, 1)))
-            run(zquant(0), constants3())
-        score(0)
-        plain(0)
-        picks(1)
-        run(cand(1, (0, 1)))
-        run(prep(0), cand(1, (2, 3)))
-        alone(0, TILES[0])
-        run(zquant(1))
-        score(1)
-        z, p = compare(0, OWN), prep(1)
-        next(z)
-        next(p)
-        plain(1)
-        alone(0, TILES[LAST])
-        next(z)
-        next(p)
-        run(z)
-        run(p)
-        addup(0)
-        alone(1, TILES[0])
-        downs = [down(0, j) for j in [0] + REST]
         if r:
-            downs.insert(0, origins_in(r - 1, False))
-        run(*downs)
-        run(down(0, LAST))
-        alone(1, TILES[LAST])
-        run(survive(0, r), compare(1, OWN))
-        addup(1)
-        for j in [0] + REST + [LAST]:
-            run(down(1, j))
+            side("sq", "sp")
+        picks(0, "sq", "sp")
+        score(0)
+        cand(1)
+        prep(0)
+        score(1)
+        pairs(0)
+        prep(1)
+        if r:
+            origins_in(r - 1, False)
         origins(0)
         origins(1)
-        run(survive(1, r), places(0))
+        survive(0, r)
+        places(0)
+        pairs(1)
+        survive(1, r)
+        places(1)
+        origins_out(r)
         if r == 0:
-            quant(T.eq[:, :], T.es[:, :], T.et[:, :], ["et%d" % b for b in range(4)], ["eq"])
-        run(renew(0, r), chain(places(1), origins_out(r)))
-        if r == 0:
-            quant(T.vq[:, :], T.vs[:, :], T.vt[:, :], ["vt"], ["vq"])
+            quant(T.eq[:, :], T.es[:, :], T.et[:, :], 512, ["et%d" % b for b in range(4)], ["eq"])
+            quant(T.vq[:, :], T.vs[:, :], T.vt[:, :], 128, ["vt"], ["vq"])
+        renew(0, r)
         if r < R - 1:
-            run(cand(0, (0, 1, 2, 3)))
-            run(zquant(0))
-        run(renew(1, r))
+            side("sl", "sm")
+            picks(1, "sl", "sm")
+            cand(0)
+        renew(1, r)
 
-    quant(T.sq[:, :], T.sp[:, :], T.bt[:, :], HALF[0] + HALF[1], ["sq"])
+    side("sq", "sp")
     dma("Y", T.oc[:, :], T.sq[:, :].bitcast(dt.uint8), ["sq"], [], "do")
-    mm("pw0", T.pw[:, 0:128], T.vq[:, :], T.vs[:, :], T.sq[:, :], T.sp[:, :], ["vq", "sq"])
-    act(T.yo[:, :], T.pw[:, 0:128], AF.Copy, [], ["yo"], ["pw0"])
+    mm("pw0", T.pw[:, 0:128], T.vq[:, :], T.vs[:, :], T.sq[:, :], T.sp[:, :], 128, ["vq", "sq"])
+    act(T.yo[:, :], T.pw[:, 0:128], AF.Copy, 128, [], ["yo"], ["pw0"])
     dma("S", T.y[:, :], T.yo[:, :], ["yo"], [], "dy")
     for k in range(4):
         dma("Y", T.osc[4 * k:4 * k + 4, :], T.sp[32 * k:32 * k + 4, :], ["sq"], [], "do")
-    run(origins_in(R - 1, True))
-    for k in sorted(cnt):
-        wait("G", k, cnt[k])
+    origins_in(R - 1, True)
+    issue()

from concourse.bass import DstId, RemoteDMATransfer
from concourse.mybir import dt, AluOpType, ActivationFunctionType

N, C, A, R = 8, 320, 64, 3
BIG = 2.0 ** 90
TILES = [[19, 18, 17], [16, 15, 14, 13], [12, 11, 10, 9], [8, 7, 6, 5], [4, 3, 2, 1]]
WIDE = [C, 256, 192, 128, 128]
NT = len(TILES)
AT = [sum(WIDE[:j]) for j in range(NT + 1)]
WHERE = {c: (j, t) for j in range(NT) for t, c in enumerate(TILES[j])}
STEP, NEAR, SHIFT = 32767, 29000, 1536
ALONE = [[0, 2], [0, 2]]
CYC, WAKE, LEAD = 0.00083, 0.16, 5.5

SCRATCH = {}


def sbuf(kind, **names):
    for k, n in names.items():
        SCRATCH[k] = ("sbuf", [128, n], kind)


BF, F4, I4, U2, Q8, U1 = "bfloat16", "float32", "int32", "uint16", "float8_e4m3fn_x4", "uint8"
sbuf(I4, li=80, lj=80, lk=80, pki=16, qi=4, qj=4, oi=64, oj=128)
sbuf(U2, op=40, pk=16, off=320, ou=64 * R, on=64 * R)
sbuf(BF, xt=4 * C, lr=512, bt=512, vt=512, et=2048, aw=1536, i8=512, zz=512, jk=8 * C, sg=8 * C)
sbuf(Q8, vq=128, eq=512, aq=384, zc=128, wq=512, sq=128, sl=128, st=256)
sbuf(U1, vs=128, es=512, ax=384, zp=128, wp=512, sp=128, sm=128, ss=256)
sbuf(F4, rb=512, yo=128, qf=4, qc=8, r16=C, r4=A, i4=C, m16=C, mb=C, rst=C, h16=C, d16=C, d4=A, olf=128, olo=64, ohi=64, osm=64, of=128)
SCRATCH["pd"] = ("psum", [128, 2048], F4)
SCRATCH["pw"] = ("psum", [128, 2048], F4)
for _f in "01":
    sbuf(BF, **{"xg" + _f: 4 * C, "zt" + _f: 4 * C, "pl" + _f: 512, "ft" + _f: 512, "ut" + _f: 4 * AT[NT]})
    sbuf(F4, **{"mk" + _f: C, "sc" + _f: C, "nt" + _f: 20, "rk" + _f: 20, "rr" + _f: 20, "rs" + _f: 20, "dd" + _f: C,
                "cc" + _f: 20, "ce" + _f: 20, "ow" + _f: C, "od" + _f: 20, "oe" + _f: 20,
                "inv" + _f: C, "en" + _f: A, "gn" + _f: A, "oz" + _f: C})
    sbuf(U2, **{"ro" + _f: 20, "of4" + _f: 16, "eo" + _f: 4})
    sbuf(Q8, **{"zq" + _f: C, "uq" + _f: AT[NT], "fq" + _f: 128, "pc" + _f: 128 * R, "lc" + _f: 256})
    sbuf(U1, **{"zs" + _f: C, "us" + _f: AT[NT], "fs" + _f: 128, "pp" + _f: 128 * R, "lp" + _f: 256})
SEMAPHORES = ["sV", "sS", "sT", "sG", "ls", "dl", "d0", "dx", "dw", "dv", "dz", "dy", "do", "ao0", "ao1", "ao2"]
SEMAPHORES += ["ar%d%d" % (_f, _r) for _f in range(2) for _r in range(R)]


def rank_program(g, core, T, topo):
    rank = T.rank_of(core)
    if rank is None:
        return
    OP, AF = AluOpType, ActivationFunctionType
    Q = {"V": g.vector, "S": g.scalar, "T": g.tensor, "G": g, "Y": g.sync}
    calls, lastw, readers, banks, total = [], {}, {}, {}, {}

    def add(e, f, rd, wr, ps, took, key, n, first=()):
        deps, after, i = set(first), set(), len(calls)
        for r in list(rd) + list(wr):
            if r in lastw:
                deps.add(lastw[r])
        for w in wr:
            deps.update(readers.get(w, []))
        for p in ps:
            for j in banks.get(p, []):
                if calls[j]["e"] != e:
                    deps.add(j)
                elif e == "T":
                    after.add(j)
            banks.setdefault(p, []).append(i)
        for r in rd:
            readers.setdefault(r, []).append(i)
        for w in wr:
            lastw[w], readers[w] = i, []
        calls.append({"e": e, "f": f, "deps": deps, "after": after - deps, "took": took, "key": key})
        total[key] = total.get(key, 0) + n
        return i

    def op(e, f, rd, wr, ps, took):
        add(e, f, rd, wr, ps, took, "s" + e, 1)

    def took(w, ind):
        return 0.05 + w * CYC * 1.3 if ind else max(64, w) * CYC

    def tt(o, a, b, how, w, rd, wr, ps=(), ind=False):
        op("V", lambda q: q.tensor_tensor(o, a, b, how), rd, wr, ps, took(w if ps or ind else 2 * w, ind))

    def ts(o, a, s1, s2, o1, o2, w, rd, wr, ps=(), ind=False):
        if o2 is None:
            op("V", lambda q: q.tensor_scalar(o, a, s1, None, o1), rd, wr, ps, took(w, ind))
        else:
            op("V", lambda q: q.tensor_scalar(o, a, s1, s2, o1, o2), rd, wr, ps, took(w, ind))

    def tc(o, a, w, rd, wr, ps=(), ind=False):
        op("V", lambda q: q.tensor_copy(o, a), rd, wr, ps, took(w, ind))

    def fill(o, v, w, wr):
        op("V", lambda q: q.memset(o, v), [], wr, (), took(w / 2, False))

    def scan(o, a, b, first, o1, o2, w, rd, wr, ps=()):
        op("V", lambda q: q.tensor_tensor_scan(o, a, b, first, o1, o2), rd, wr, ps, took(w, False))

    def quant(c, s, t, w, rd, wr):
        op("V", lambda q: q.quantize_mx(c, s, t), rd, wr, (), 0.012 + 0.00088 * w)

    def act(o, i, func, w, rd, wr, ps=(), ind=False, **kw):
        op("S", lambda q: q.activation(o, i, func, **kw), rd, wr, ps, took(w, ind))

    def mm(bank, o, w, ws, x, xs, n, rd, start=True, stop=True):
        op("T", lambda q: q.matmul_mx(o, w, ws, x, xs, start, stop), rd, [], [bank], (n + 16) * 0.001)

    def dma(e, out, in_, rd, wr, k, took=2.2):
        i = add(e, lambda q: q.dma_start(out, in_), rd, wr, (), 0.06, None, 0)
        j = add("A", None, [], wr, (), took, k, 16, [i])
        calls[i]["lands"] = j
        for r in rd:
            readers[r].append(j)

    def iota(o, pattern, base, mult, w, wr, **kw):
        op("G", lambda q: q.iota(o, pattern, base, mult, **kw), [], wr, (), 0.13 + 2 * w * CYC)

    def send(f, rd, keys):
        for k, n in keys:
            total[k] = total.get(k, 0) + n
        return add("G", f, rd, [], (), 0.9, None, 0)

    def came(first, wr, k, more=0.0):
        calls[add("A", None, [], wr, (), 2.0, k, 0, first)]["more"] = more

    def issue():
        n, names = len(calls), list(Q) + ["A"]
        users, left, far, early = [[] for _c in calls], [0] * n, [0.0] * n, [0.0] * n
        for i, c in enumerate(calls):
            for j in sorted(c["deps"] | c["after"]):
                users[j].append(i)
                left[i] += 1

        def later(i, j):
            return 0.0 if i in calls[j]["after"] else WAKE

        for i in range(n - 1, -1, -1):
            far[i] = calls[i]["took"] + calls[i].get("more", 0.0)
            far[i] += max([far[j] + later(i, j) for j in users[i]], default=0.0)
        ready, free, line = {e: [] for e in names}, {e: 0.0 for e in names}, []
        for i in range(n):
            if not left[i]:
                ready[calls[i]["e"]].append(i)
        while len(line) < n:
            best = None
            for e in names:
                if ready[e]:
                    i = min(ready[e], key=lambda j: early[j])
                    t = early[i]
                    if e != "A":
                        t = max(t, free[e])
                        i = max((j for j in ready[e] if early[j] <= t), key=lambda j: (far[j], -j))
                    if best is None or t < best[0]:
                        best = (t, i)
            t, i = best
            e = calls[i]["e"]
            ready[e].remove(i)
            line.append(i)
            free[e] = t + calls[i]["took"]
            for j in users[i]:
                left[j] -= 1
                early[j] = max(early[j], free[e] + later(i, j))
                if not left[j]:
                    ready[calls[j]["e"]].append(j)
        cnt, seen, snap, tok = {}, {e: {} for e in Q}, {}, {}

        def wait(e, k, m):
            if seen[e].get(k, 0) < m:
                Q[e].wait_ge(T.sem[k], m)
                seen[e][k] = m
                for a, b in snap.get((k, m), {}).items():
                    if seen[e].get(a, 0) < b:
                        seen[e][a] = b

        for i in line:
            c = calls[i]
            e, want = c["e"], {}
            if e == "A":
                tok[i] = (c["key"], total[c["key"]])
                continue
            for j in c["deps"]:
                if j in tok:
                    k, m = tok[j]
                    want[k] = max(m, want.get(k, 0))
            for k in sorted(want):
                wait(e, k, want[k])
            x = c["f"](Q[e])
            if c["key"]:
                k = c["key"]
                cnt[k] = cnt.get(k, 0) + 1
                x.then_inc(T.sem[k], 1)
                tok[i] = (k, cnt[k])
                snap[tok[i]] = dict(seen[e])
            elif "lands" in c:
                x.then_inc(T.sem[calls[c["lands"]]["key"]], 16)
        for k in sorted(k for k in total if k):
            wait("G", k, total[k])

    HALF = [["b%d%d" % (h, b) for b in range(4)] for h in range(2)]
    LI = ["li0", "li1", "li2", "li3"]

    for i, nm in enumerate(("la", "lx", "ra", "rx")):
        dma("S", T.li[:, 20 * i:20 * i + 20], T[nm][:, :], [], [LI[i]], "dl")
    dma("Y", T.lr[:, 0:256], T.l0[:, :], [], ["lr0"], "d0")
    dma("Y", T.lr[:, 256:512], T.r0[:, :], [], ["lr1"], "d0")
    dma("Y", T.xt[:, :], T.x[:, :], [], ["xt"], "dx", 3.0)
    dma("Y", T.wq[:, :].bitcast(dt.uint8), T.wc[:, :], [], ["wq"], "dw", 4.0)
    dma("Y", T.wp[:, :], T.ws[:, :], [], ["wp"], "dw", 4.0)
    dma("Y", T.vt[:, :], T.v[:, :], [], ["vt"], "dv", 5.0)

    big = {"allow_small_or_imprecise_dtypes": True}
    iota(T.qi[:, 3:4], [[1, 1]], 0, 1, 1, ["qi"])
    iota(T.pki[:, 0:8], [[8, 8]], 64, 0, 8, ["pki"])
    iota(T.pki[:, 8:16], [[8, 8]], 0, 0, 8, ["pki2"])
    iota(T.r16[:, :], [[0, 20], [STEP, 16]], 0, 0, C, ["r16"], **big)
    iota(T.r4[:, :], [[0, 16], [STEP, 4]], 0, 0, A, ["r4"], **big)
    iota(T.i8[:, :], [[1, 8], [0, 64]], 0, 0, 512, ["i8"], **big)
    runs = [[], []]
    for f in range(2):
        al = [c for j in ALONE[f] for c in TILES[j]]
        val = [2 * (16 * (19 - c) - 8 * sum(a > c for a in al) + 15) + (16 * c if c in al else 0) - 15 * SHIFT for c in range(20)]
        c = 0
        while c < 20:
            d, e = (val[c + 1] - val[c] if c < 19 else 0), c + 1
            while e < 20 and val[e] - val[e - 1] == d:
                e += 1
            runs[f].append("cc%d%d" % (f, c))
            iota(T["cc%d" % f][:, c:e], [[d, e - c]], val[c], 0, e - c, [runs[f][-1]], **big)
            c = e
    iota(T.i4[:, :], [[4, C]], 0, 0, C, ["i4"], **big)
    iota(T.olf[:, :], [[32, 2], [0, 2], [1, 32]], 0, 0, 128, ["olf"], **big)
    fill(T.zz[:, :], 0.0, 512, ["zz"])

    def column(b):
        o = T.et[:, 512 * b:512 * b + 512]
        op("G", lambda q: q.affine_select(o, T.zz[:, :], [[1, 512]], OP.not_equal, 0.5, -b, -4), ["zz"], ["et%d" % b], (), 1.02)

    for b in range(4):
        column(b)
    quant(T.zc[:, :], T.zp[:, :], T.zz[:, :], 128, ["zz"], ["zc"])
    for f in range(2):
        u = "%d" % f
        dma("Y", T["lc" + u][:, 0:64].bitcast(dt.uint8), T.zc[:, 0:64].bitcast(dt.uint8), ["zc"], ["pad" + u], "dz")
        dma("Y", T["lp" + u][:, 0:64], T.zp[:, 0:64], ["zc"], ["pae" + u], "dz")
    tc(T.pk[:, :], T.pki[:, :], 16, ["pki", "pki2"], ["pk"])
    for f in range(2):
        u = "%d" % f
        for j in range(NT):
            a, b = 4 * (AT[j] + 16 * TILES[j][-1]), 4 * AT[j + 1]
            fill(T["ut" + u][:, a:b], 0.0, b - a, ["u%d%d%d" % (f, j, t) for t in range(4)])
        fill(T["pl" + u][:, 256:512], 0.0, 256, ["pz" + u])
        fill(T["ft" + u][:, 256:512], 0.0, 256, ["fz" + u])
        fill(T["rk" + u][:, 0:1], 0.0, 1, ["rk%s0" % u])
    ts(T.qj[:, 0:1], T.qi[:, 3:4], 15, None, OP.bitwise_and, None, 1, ["qi"], ["qj0"])
    ts(T.qj[:, 1:2], T.qi[:, 3:4], 2, 3, OP.logical_shift_right, OP.bitwise_and, 1, ["qi"], ["qj1"])
    ts(T.qj[:, 2:3], T.qi[:, 3:4], 3, None, OP.bitwise_and, None, 1, ["qi"], ["qj2"])
    ts(T.qj[:, 3:4], T.qi[:, 3:4], 4, None, OP.logical_shift_right, None, 1, ["qi"], ["qj3"])
    tc(T.qf[:, :], T.qj[:, :], 4, ["qj0", "qj1", "qj2", "qj3"], ["qf"])
    ts(T.qc[:, 0:1], T.qf[:, 0:1], float(STEP), None, OP.mult, None, 1, ["qf"], ["qc0"])
    ts(T.qc[:, 1:2], T.qf[:, 0:1], float(STEP), float(NEAR), OP.mult, OP.add, 1, ["qf"], ["qc1"])
    ts(T.qc[:, 2:3], T.qf[:, 1:2], float(STEP), float(NEAR), OP.mult, OP.add, 1, ["qf"], ["qc2"])
    ts(T.m16[:, :], T.r16[:, :], T.qc[:, 0:1], 2 * BIG, OP.is_equal, OP.mult, C, ["r16", "qc0"], ["m16"])
    ts(T.mb[:, :], T.m16[:, :], -BIG, None, OP.add, None, C, ["m16"], ["mb"])
    ts(T.h16[:, :], T.r16[:, :], 0.0, None, OP.is_gt, None, C, ["r16"], ["h16"])
    ts(T.rst[:, :], T.h16[:, :], 2 * BIG, -BIG, OP.mult, OP.add, C, ["h16"], ["rst"])
    ts(T.d16[:, :], T.r16[:, :], T.qc[:, 1:2], float(SHIFT), OP.subtract, OP.min, C, ["r16", "qc1"], ["d16"])
    ts(T.d4[:, :], T.r4[:, :], T.qc[:, 2:3], float(SHIFT), OP.subtract, OP.min, A, ["r4", "qc2"], ["d4"])
    ts(T.qc[:, 3:4], T.qf[:, 0:1], float(SHIFT), -15.0 * SHIFT, OP.mult, OP.add, 1, ["qf"], ["qc3"])
    ts(T.qc[:, 4:5], T.qf[:, 1:2], float(SHIFT), T.qf[:, 2:3], OP.mult, OP.add, 1, ["qf"], ["qc4"])
    ts(T.qc[:, 5:6], T.qf[:, 0:1], float(SHIFT - 2), None, OP.mult, None, 1, ["qf"], ["qc5"])
    for f in range(2):
        ts(T["ce%d" % f][:, :], T["cc%d" % f][:, :], T.qc[:, 5:6], None, OP.add, None, 20, runs[f] + ["qc5"], ["ce%d" % f])
    ts(T.aw[:, 512:1024], T.i8[:, :], T.qf[:, 3:4], -2.0, OP.is_equal, OP.mult, 512, ["i8", "qf"], ["aw1"])
    act(T.aw[:, 0:512], T.aw[:, 512:1024], AF.Copy, 512, ["aw1"], ["aw0"], scale=0.5)
    act(T.aw[:, 3:512:4], T.aw[:, 515:1024:4], AF.Copy, 128, ["aw1"], ["aw0"])
    act(T.aw[:, 1024:1536], T.aw[:, 512:1024], AF.Copy, 512, ["aw1"], ["aw2"], scale=0.5)
    quant(T.aq[:, :], T.ax[:, :], T.aw[:, :], 384, ["aw0", "aw1", "aw2"], ["aq"])
    for t in range(4):
        ts(T.off[:, 80 * t:80 * t + 80], T.li[:, :], 4.0, float(t), OP.mult, OP.add, 80, LI, ["ot%d" % t])
    ts(T.lj[:, :], T.li[:, :], 32.0, 32.0, OP.is_ge, OP.mult, 80, LI, ["lj"])
    tt(T.lk[:, :], T.lj[:, :], T.li[:, :], OP.add, 80, ["lj"] + LI, ["lk"])
    tc(T.op[:, 0:20], T.lk[:, 0:20], 20, ["lk"], ["op0"])
    ts(T.op[:, 20:40], T.lk[:, 40:60], 32.0, None, OP.add, None, 20, ["lk"], ["op1"])
    act(T.bt[:, 0:256], T.lr[:, 0:256], AF.Copy, 256, ["lr0"], HALF[0], scale=0.5)
    act(T.bt[:, 256:512], T.lr[:, 256:512], AF.Copy, 256, ["lr1"], HALF[1], scale=0.5)

    def xgather(e, f, t):
        o = T["xg%d" % f][:, C * t:C * t + C]
        w = T.xt[:, :].indirect(T.off[:, 80 * t + 40 * f + 20:80 * t + 40 * f + 40])
        if e == "S":
            act(o, w, AF.Copy, C, ["xt", "ot%d" % t], ["xg%d%d" % (f, t)], (), True, scale=0.5)
        else:
            ts(o, w, 0.5, None, OP.mult, None, C, ["xt", "ot%d" % t], ["xg%d%d" % (f, t)], (), True)

    def side(q, x):
        quant(T[q][:, :], T[x][:, :], T.bt[:, :], 128, HALF[0] + HALF[1], [q])

    def picks(f, q, x):
        s, k = slice(128 * f, 128 * f + 128), T.pk[:, 8 * f:8 * f + 8]
        tc(T.st[:, s].bitcast(dt.uint32), T[q][:, 0:128].bitcast(dt.uint32).indirect(k), 128, [q, "pk"], ["st%d" % f], (), True)
        act(T.ss[:, s], T[x][:, 0:128].indirect(k), AF.Copy, 128, [q, "pk"], ["ss%d" % f], (), True)

    def cand(f):
        u = "%d" % f
        for t in range(4):
            w = T.bt[:, 256 * f:256 * f + 256].indirect(T.off[:, 80 * t + 40 * f:80 * t + 40 * f + 20])
            tt(T["zt" + u][:, t:4 * C:4], w, T["xg" + u][:, C * t:C * t + C], OP.add, C, HALF[f] + ["ot%d" % t, "xg%d%d" % (f, t)], ["zt%d%d" % (f, t)], (), True)
        quant(T["zq" + u][:, :], T["zs" + u][:, :], T["zt" + u][:, :], C, ["zt" + u + "%d" % t for t in range(4)], ["zq" + u])

    def score(f):
        u = "%d" % f
        s = slice(128 * f, 128 * f + 128)
        for b in ("pw", "pd"):
            mm(b + u, T[b][:, 512 * f:512 * f + C], T.st[:, s], T.ss[:, s], T["zq" + u][:, :], T["zs" + u][:, :], C, ["st" + u, "ss" + u, "zq" + u])

    def slot(f, c):
        j, t = WHERE[c]
        return T["ut%d" % f][:, 4 * AT[j] + t:4 * (AT[j] + 16 * c):4], ["u%d%d%d" % (f, j, t)]

    def prep(f):
        u = "%d" % f
        k, o = T.pw[:, 512 * f:512 * f + C], T["ut" + u][:, 3:4 * C:4]
        tt(T["mk" + u][:, :], k, T.mb[:, :], OP.min, C, ["mb"], ["mk" + u], ["pw" + u])
        scan(T["sc" + u][:, :], T.rst[:, :], T["mk" + u][:, :], -BIG, OP.min, OP.max, C, ["rst", "mk" + u], ["sc" + u])
        act(T["nt" + u][:, :], T["sc" + u][:, 15:C:16], AF.Copy, 20, ["sc" + u], ["nt" + u], scale=-1.0)
        tt(o, k, T["sc" + u][:, :], OP.is_gt, C, ["sc" + u], ["u%d03" % f], ["pw" + u])
        scan(T["ow" + u][:, :], T.h16[:, :], o, 0.0, OP.mult, OP.add, C, ["h16", "u%d03" % f], ["ow" + u])
        act(T["od" + u][:, :], T["ow" + u][:, 15:C:16], AF.Copy, 20, ["ow" + u], ["od" + u], scale=2.0)
        tt(T["oe" + u][:, :], T["od" + u][:, :], T["ce" + u][:, :], OP.add, 20, ["od" + u, "ce" + u], ["oe" + u])

    turn = [0, 0]

    def pairs(f):
        u = "%d" % f
        for j in range(NT):
            for c in TILES[j]:
                w = 16 * c
                k = T["pd" if j in ALONE[f] else "pw"][:, 512 * f:512 * f + w]
                o, n = slot(f, c)
                if j in ALONE[f]:
                    m, turn[0] = turn[0] % 8, turn[0] + 1
                    x = T.sg[:, C * m:C * m + w]
                    act(x, k, AF.Sign, w, ["nt" + u], ["sg%d" % m], ["pd" + u], bias=T["nt" + u][:, c:c + 1])
                    act(o, x, AF.Sign, w, ["sg%d" % m], n + ["rk%s%d" % (u, c)], bias=0.5, accum_out=T["rk" + u][:, c:c + 1])
                else:
                    m, turn[1] = turn[1] % 8, turn[1] + 1
                    ts(o, k, T["sc" + u][:, w + 15:w + 16], None, OP.is_ge, None, w, ["sc" + u], n, ["pw" + u])
                    act(T.jk[:, C * m:C * m + w], o, AF.Copy, w, n, ["jk%d" % m, "rk%s%d" % (u, c)], scale=2.0, accum_out=T["rk" + u][:, c:c + 1])
            s = slice(AT[j], AT[j + 1])
            quant(T["uq" + u][:, s], T["us" + u][:, s], T["ut" + u][:, 4 * AT[j]:4 * AT[j + 1]], WIDE[j], ["u%d%d%d" % (f, j, t) for t in range(4)], ["uq%s%d" % (u, j)])
            b, w = 2 + f, 128 if j not in ALONE[f] else 256 if j else 0
            mm("pw%d" % b, T.pw[:, 512 * b:512 * b + WIDE[j]], T.aq[:, w:w + 128], T.ax[:, w:w + 128], T["uq" + u][:, s], T["us" + u][:, s],
               WIDE[j], ["aq", "uq%s%d" % (u, j)], j == 0, j == NT - 1)

    def survive(f, r):
        u = "%d" % f
        n = "%d%d" % (f, r)
        b = 2 + f
        tt(T["rr" + u][:, :], T["rk" + u][:, :], T["oe" + u][:, :], OP.add, 20, ["rk%d%d" % (f, c) for c in range(20)] + ["oe" + u], ["rr" + u])
        scan(T["dd" + u][:, :], T.d16[:, :], T.pw[:, 512 * b:512 * b + C], 0.0, OP.add, OP.max, C, ["d16"], ["dd" + u], ["pw%d" % b])
        tt(T["rs" + u][:, :], T["rr" + u][:, :], T["dd" + u][:, 15:C:16], OP.add, 20, ["rr" + u, "dd" + u], ["rs" + u])
        ts(T["ro" + u][:, :], T["rs" + u][:, :], 0.5, None, OP.mult, None, 20, ["rs" + u], ["ro" + u])
        tc(T["inv" + u][:, :].indirect(T["ro" + u][:, 0:20]), T.i4[:, :], 2.4 * C, ["ro" + u, "i4"], ["inv" + u], (), True)
        scan(T["gn" + u][:, :], T.d4[:, :], T["inv" + u][:, 0:A], 0.0, OP.add, OP.max, A, ["inv" + u, "d4"], ["gn" + u])
        ts(T["of4" + u][:, :], T["gn" + u][:, 3:A:4], T.qc[:, 4:5], -3.0 * SHIFT, OP.add, OP.add, 16, ["gn" + u, "qc4"], ["of4" + u])
        tc(T["pl" + u][:, 0:256], T["zt" + u][:, :].indirect(T["of4" + u][:, 0:16]), 256, ["of4" + u] + ["zt" + u + "%d" % t for t in range(4)], ["pl" + u], (), True)
        v = slice(128 * r, 128 * r + 128)
        quant(T["pc" + u][:, v], T["pp" + u][:, v], T["pl" + u][:, :], 128, ["pl" + u, "pz" + u], ["pc" + n])
        d = T.cores[(rank + 1 - 2 * f) % N]
        rid, pid = topo.addr(d, core)
        m, ne = topo.mask(core, d), len(topo.engines(core, d))
        s, v, k = slice(64 * r + 64, 64 * r + 128), slice(128 * r, 128 * r + 64), "ar" + n
        keys = [("ls", ne), (k, ne)]
        i = send(lambda q: q.remote_dma(T["lc" + u][:, s].bitcast(dt.uint8), T["pc" + u][:, v].bitcast(dt.uint8), T.sem[k], T.sem.ls, pid, rid, m), ["pc" + n], keys)
        j = send(lambda q: q.remote_dma(T["lp" + u][:, s], T["pp" + u][:, v], T.sem[k], T.sem.ls, pid, rid, m), ["pc" + n], keys)
        came([i, j], ["lc" + n], k, LEAD * (1 - f))

    def places(f):
        u = "%d" % f
        scan(T["en" + u][:, :], T.d16[:, 0:A], T["inv" + u][:, 0:A], 0.0, OP.add, OP.max, A, ["inv" + u, "d16"], ["en" + u])
        ts(T["eo" + u][:, :], T["en" + u][:, 15:A:16], T.qc[:, 3:4], 0.25, OP.add, OP.mult, 4, ["en" + u, "qc3"], ["eo" + u])
        s = slice(32 * f, 32 * f + 32)
        act(T.olo[:, s], T["oz" + u][:, :].indirect(T["eo" + u][:, 0:2]), AF.Copy, 32, ["oz" + u, "eo" + u], ["olo" + u], (), True)
        act(T.ohi[:, s], T["oz" + u][:, :].indirect(T["eo" + u][:, 2:4]), AF.Copy, 32, ["oz" + u, "eo" + u], ["ohi" + u], (), True, scale=64.0)

    def origins(f):
        act(T["oz%d" % f][:, :], T.olf[:, :].indirect(T.op[:, 20 * f:20 * f + 20]), AF.Copy, C, ["olf", "op%d" % f], ["oz%d" % f], (), True)

    def origins_out(r):
        n = "%d" % r
        tt(T.osm[:, :], T.olo[:, :], T.ohi[:, :], OP.add, 64, ["olo0", "olo1", "ohi0", "ohi1"], ["osm"])
        tc(T.ou[:, 64 * r:64 * r + 64], T.osm[:, :], 64, ["osm"], ["ou" + n])
        tr, keys = [], []
        for f in range(2):
            d = T.cores[(rank + 1 - 2 * f) % N]
            rid, pid = topo.addr(d, core)
            en = topo.engines(core, d)
            h, s = len(en) // 2, slice(64 * r + 32 * f, 64 * r + 32 * f + 32)
            tr.append(RemoteDMATransfer(dst_ids=[DstId(rid=rid, pnc=pid)], dma_engine_mask=sum(1 << e for e in en[h * f:h * f + h]),
                                        remote_sem=T.sem["ao" + n], src=T.ou[:, s], dst=T.on[:, s]))
            keys += [("ls", h), ("ao" + n, h)]
        i = send(lambda q: q.remote_dma_fused(tr, local_sem=T.sem.ls), ["ou" + n], keys)
        came([i], ["on" + n], "ao" + n)

    def origins_in(r, last):
        n = "%d" % r
        tc(T.oi[:, :], T.on[:, 64 * r:64 * r + 64], 64, ["on" + n], ["oi"])
        ts(T.oj[:, 0:64], T.oi[:, :], 63, None, OP.bitwise_and, None, 64, ["oi"], ["oj0"])
        ts(T.oj[:, 64:128], T.oi[:, :], 6, None, OP.logical_shift_right, None, 64, ["oi"], ["oj1"])
        if not last:
            tc(T.olf[:, :], T.oj[:, :], 128, ["oj0", "oj1"], ["olf"])
            return
        for f in range(2):
            base = float(A * ((rank - R + 2 * R * f) % N))
            for h in range(2):
                o, i = 64 * f + 32 * h, 64 * h + 32 * f
                ts(T.of[:, o:o + 32], T.oj[:, i:i + 32], base, None, OP.add, None, 32, ["oj%d" % h], ["of%d%d" % (f, h)])
        dma("Y", T.ot[:, :], T.of[0:128:16, :], ["of00", "of01", "of10", "of11"], [], "do")

    def renew(h, r):
        last, u = r == R - 1, "%d" % h
        n = "%d%d" % (h, r)
        W = [slice(128 * b, 128 * b + 128) for b in range(4)]
        P = [slice(512 * b, 512 * b + 128) for b in range(4)]
        D = [slice(512 * b + 64, 512 * b + 128) for b in range(4)]
        K = [slice(512 * b, 512 * b + 64) for b in range(4)]
        B = [slice(64 * b + 256 * h, 64 * b + 256 * h + 64) for b in range(4)]
        x, ft = slice(64 * r, 64 * r + 128), T["ft" + u]
        two = 2.0 if last else 1.0
        for b in range(4):
            mm("pd%d" % b, T.pd[:, P[b]], T.eq[:, W[b]], T.es[:, W[b]], T["lc" + u][:, x], T["lp" + u][:, x], 128, ["lc" + n, "eq", "pad" + u, "pae" + u])
        for b in range(4):
            o, i = ft[:, b:256:4], T.pd[:, D[b]]
            if b % 2:
                act(o, i, AF.Copy, 64, [], ["ft%s%d" % (u, b)], ["pd%d" % b], scale=two)
            else:
                ts(o, i, two, None, OP.mult, None, 64, [], ["ft%s%d" % (u, b)], ["pd%d" % b])
        quant(T["fq" + u][:, :], T["fs" + u][:, :], ft[:, :], 128, ["ft%s%d" % (u, b) for b in range(4)] + ["fz" + u], ["fq" + u])
        for b in range(4):
            mm("pw%d" % b, T.pw[:, P[b]], T.wq[:, W[b]], T.wp[:, W[b]], T["fq" + u][:, :], T["fs" + u][:, :], 128, ["wq", "wp", "fq" + u])
        for b in range(4):
            act(T.rb[:, B[b]], T.pw[:, K[b]], AF.Relu, 64, [], ["rb%s%d" % (u, b)], ["pw%d" % b], scale=0.03125)
        for b in range(4):
            o, i = T.bt[:, 256 * h + b:256 * h + 256:4], T.rb[:, B[b]]
            if last:
                tt(o, i, ft[:, b:256:4], OP.add, 64, ["rb%s%d" % (u, b), "ft%s%d" % (u, b)], ["b%s%d" % (u, b)])
            else:
                tt(o, i, T.pd[:, D[b]], OP.add, 64, ["rb%s%d" % (u, b)], ["b%s%d" % (u, b)], ["pd%d" % b])

    for t in range(4):
        xgather("S" if t < 2 else "V", 0, t)
    for t in range(4):
        xgather("S", 1, t)
    cand(0)
    side("sq", "sp")
    picks(1, "sq", "sp")
    for r in range(R):
        if r:
            side("sq", "sp")
        picks(0, "sq", "sp")
        score(0)
        cand(1)
        prep(0)
        score(1)
        pairs(0)
        prep(1)
        if r:
            origins_in(r - 1, False)
        origins(0)
        origins(1)
        survive(0, r)
        places(0)
        pairs(1)
        survive(1, r)
        places(1)
        origins_out(r)
        if r == 0:
            quant(T.eq[:, :], T.es[:, :], T.et[:, :], 512, ["et%d" % b for b in range(4)], ["eq"])
            quant(T.vq[:, :], T.vs[:, :], T.vt[:, :], 128, ["vt"], ["vq"])
        renew(0, r)
        if r < R - 1:
            side("sl", "sm")
            picks(1, "sl", "sm")
            cand(0)
        renew(1, r)

    side("sq", "sp")
    dma("Y", T.oc[:, :], T.sq[:, :].bitcast(dt.uint8), ["sq"], [], "do")
    mm("pw0", T.pw[:, 0:128], T.vq[:, :], T.vs[:, :], T.sq[:, :], T.sp[:, :], 128, ["vq", "sq"])
    act(T.yo[:, :], T.pw[:, 0:128], AF.Copy, 128, [], ["yo"], ["pw0"])
    dma("S", T.y[:, :], T.yo[:, :], ["yo"], [], "dy")
    for k in range(4):
        dma("Y", T.osc[4 * k:4 * k + 4, :], T.sp[32 * k:32 * k + 4, :], ["sq"], [], "do")
    origins_in(R - 1, True)
    issue()
